import numpy as np
import ml_dtypes


def mxq(x, axis, fmt="e4m3"):
    dtype, down = {"e4m3": (ml_dtypes.float8_e4m3fn, 7), "e5m2": (ml_dtypes.float8_e5m2, 14)}[fmt]
    v = np.moveaxis(np.asarray(x, np.float32).astype(ml_dtypes.bfloat16).astype(np.float64), axis, -1)
    blocks = v.reshape(v.shape[:-1] + (-1, 32))
    amax = np.abs(blocks).max(-1, keepdims=True)
    byte = np.maximum(np.where(amax > 0, np.frexp(amax)[1] - 1 + 127, 0) - down, 1)
    scale = np.exp2(byte - 127.0)
    codes = (blocks / scale).astype(np.float32).astype(dtype).astype(np.float64)
    return np.moveaxis((codes * scale).reshape(v.shape), -1, axis)


WIDE = False


def mx_kscale(k):
    if not WIDE:
        return np.ones(k)
    levels = np.array([10, -10, 5, -5, 0])
    if k % 512:
        return np.exp2(np.random.permutation(np.resize(levels, k // 32))).repeat(32)
    a = np.empty((k // 512, 16))
    for p in range(k // 512):
        a[p, :8] = np.random.permutation(np.resize(levels, 8))
        for g in range(8):
            far = levels[np.abs(levels - a[p, g]) >= 10]
            a[p, g + 8] = far[np.random.randint(len(far))]
    return np.exp2(a.ravel()).repeat(32)


def f64(x):
    return np.asarray(x).astype(np.float64)


def striped(idx):
    return np.tile(idx.reshape(-1, 16).T, (8, 1)).astype(np.uint16)


def unstriped(offs):
    return offs[:16].T.reshape(-1).astype(np.int64)


E2M1 = np.array([0.0, 0.5, 1.0, 1.5, 2.0, 3.0, 4.0, 6.0, -0.0, -0.5, -1.0, -1.5, -2.0, -3.0, -4.0, -6.0])


def pack_weight(w, fmt):
    k, n = w.shape
    w = f64(np.asarray(w, np.float32).astype(ml_dtypes.bfloat16)).reshape(k // 32, 32, n)
    amax = np.abs(w).max(1)
    if fmt == "e4m3":
        byte = np.frexp(amax)[1] - 1 + 127 - 7
    else:
        mant, ex = np.frexp(amax / 6.0)
        byte = np.where(mant > 0.5, ex, ex - 1) + 127
    byte = np.clip(np.where(amax > 0, byte, 1), 1, 254)
    scaled = (w * np.exp2(127.0 - byte)[:, None, :]).reshape(k, n).astype(np.float32)
    by_word = np.ascontiguousarray(scaled.reshape(k // 512, 128, 4, n).transpose(0, 1, 3, 2))
    if fmt == "e4m3":
        words = by_word.astype(ml_dtypes.float8_e4m3fn).view(np.uint8)
    else:
        c = by_word.astype(ml_dtypes.float4_e2m1fn).view(np.uint8) & 0xF
        words = (c[..., 0::2] | (c[..., 1::2] << 4)).reshape(k // 512, 128, 2 * n)
    return np.ascontiguousarray(words), np.ascontiguousarray(byte.astype(np.uint8).reshape(k // 512, 16, n))


def unpack_weight(words, scales, fmt):
    g, _, n = scales.shape
    words = np.ascontiguousarray(words).reshape(g, 128, n, -1)
    if fmt == "e4m3":
        vals = words.view(ml_dtypes.float8_e4m3fn).astype(np.float64)
    else:
        nib = np.empty((g, 128, n, 4), np.uint8)
        nib[..., 0::2] = words & 0xF
        nib[..., 1::2] = words >> 4
        vals = E2M1[nib]
    vals = vals * np.repeat(np.exp2(scales.astype(np.float64) - 127.0), 8, axis=1)[..., None]
    return vals.transpose(0, 1, 3, 2).reshape(g * 512, n)


def d_relu(v):
    return (v > 0).astype(np.float64)


K, T, E, C, H, N = 256, 1024, 6, 128, 512, 1536


def by_expert(wq, xq):
    return np.concatenate([wq[e].T @ xq[:, e * C:(e + 1) * C] for e in range(E)], axis=1)


def setup_inputs():
    n = np.random.standard_normal
    v = mx_kscale(N)
    u = mx_kscale(H)
    slot_token = np.random.permutation(T)[:E * C]
    w_slot = np.random.uniform(0.2, 1.0, E * C)
    dy = pack_weight(n((N, T)) * v[:, None], "e4m3")
    wt = pack_weight(n((N, K)) / np.sqrt(N) / v[:, None], "e4m3")
    wbt = [pack_weight(m, "e2m1") for m in n((E, N, H)) / np.sqrt(N) / v[None, :, None] * u]
    wat = [pack_weight(m, "e2m1") for m in n((E, H, K)) / np.sqrt(H) / u[None, :, None]]
    return {
        "dy_words": dy[0],
        "dy_scales": dy[1],
        "wt_words": wt[0],
        "wt_scales": wt[1],
        "wbt_words": np.stack([m[0] for m in wbt]),
        "wbt_scales": np.stack([m[1] for m in wbt]),
        "wat_words": np.stack([m[0] for m in wat]),
        "wat_scales": np.stack([m[1] for m in wat]),
        "a": (n((H, E * C))).astype(np.float32),
        "gate": (np.tile(w_slot, (128, 1))).astype(np.float32),
        "offs": striped(slot_token),
    }


def reference(dy_words, dy_scales, wt_words, wt_scales, wbt_words, wbt_scales, wat_words, wat_scales, a, gate, offs):
    wt = unpack_weight(wt_words, wt_scales, "e4m3")
    wbt = np.stack([unpack_weight(wbt_words[e], wbt_scales[e], "e2m1") for e in range(E)])
    wat = np.stack([unpack_weight(wat_words[e], wat_scales[e], "e2m1") for e in range(E)])
    idx = unstriped(offs)
    dy = unpack_weight(dy_words, dy_scales, "e4m3")
    base = wt.T @ dy
    dh = f64(gate[:1]) * by_expert(wbt, dy[:, idx]) * d_relu(f64(a))
    dx = by_expert(wat, mxq(dh, 0, "e4m3"))
    c = np.zeros((K, T))
    c[:, idx] = dx
    return base + c

@@ -1,0 +1,253 @@
+from contextlib import ExitStack
+
+import concourse.mybir as mybir
+from concourse.masks import make_identity
+
+K, T, E, C, H, N = 256, 1024, 6, 128, 512, 1536
+S = E * C
+P = 128
+PASSES = N // 512
+FLOPS = 2 * N * K * T + 2 * N * H * S + 2 * H * K * S
+
+F32 = mybir.dt.float32
+BF16 = mybir.dt.bfloat16
+I32 = mybir.dt.int32
+U32 = mybir.dt.uint32
+U16 = mybir.dt.uint16
+U8 = mybir.dt.uint8
+FP8X4 = mybir.dt.float8_e4m3fn_x4
+FP4X4 = mybir.dt.float4_e2m1fn_x4
+ACT = mybir.ActivationFunctionType
+ALU = mybir.AluOpType
+
+
+def tile_moe_adb_relu_kernel(
+    tc, dy_words, dy_scales, wt_words, wt_scales, wbt_words, wbt_scales, wat_words, wat_scales, a, gate, offs, out
+):
+    nc = tc.nc
+    with ExitStack() as ctx:
+        keep = ctx.enter_context(tc.tile_pool(name="keep", bufs=1))
+        ring = ctx.enter_context(tc.tile_pool(name="ring", bufs=3))
+        psum = ctx.enter_context(tc.psum_pool(name="psum", bufs=2))
+
+        def held(shape, dtype, name):
+            return keep.tile(shape, dtype, name=name, align_bytes=64)
+
+        offsets = keep.tile([P, S // 16], U16, name="offsets")
+        dyw = [held([P, T], I32, "dyw%d" % s) for s in range(PASSES)]
+        dys = held([P, T], U8, "dys")
+        gw = [held([P, S], I32, "gw%d" % s) for s in range(PASSES)]
+        gs = [held([P, S], U8, "gs%d" % s) for s in range(PASSES)]
+        wtw = held([P, PASSES, K], I32, "wtw")
+        wts = held([P, PASSES, K], U8, "wts")
+        wbw = [held([P, PASSES, 2 * H], U8, "wbw%d" % e) for e in range(E)]
+        wbs = held([P, E * PASSES, H], U8, "wbs")
+        waw = held([P, E, 2 * K], U8, "waw")
+        was = held([P, E, K], U8, "was")
+        a_sb = [held([P, 4, 2 * C], F32, "a%d" % g) for g in range(E // 2)]
+        gate_rows = held([P, C], F32, "gate_rows")
+        gate_col = held([P, 8], F32, "gate_col")
+        ident = held([P, P], F32, "ident")
+        dx = held([P, 2, S], F32, "dx")
+        win = [held([P, T], F32, "win%d" % kt) for kt in range(2)]
+        res = [held([P, T], F32, "res%d" % kt) for kt in range(2)]
+
+        def zero(tile2d):
+            nc.vector.memset(tile2d.bitcast(I32), 0)
+
+        zero(dys[:])
+        zero(wbs[:].rearrange("p a b -> p (a b)"))
+        zero(gs[1][:])
+        zero(gs[2][:])
+        zero(was[:].rearrange("p a b -> p (a b)"))
+        zero(wts[:].rearrange("p a b -> p (a b)"))
+        make_identity(nc, ident[:])
+        for kt in range(2):
+            nc.gpsimd.memset(win[kt][:], 0.0)
+
+        nc.sync.dma_start(offsets[:], offs)
+        nc.sync.dma_start(dyw[0][:], dy_words[0].rearrange("p t d -> p (t d)").bitcast(I32))
+        for q in range(4):
+            nc.scalar.dma_start(dys[32 * q : 32 * q + 8, :].bitcast(I32), dy_scales[0:2, 4 * q : 4 * q + 4, :].bitcast(I32))
+            nc.scalar.dma_start(dys[32 * q + 8 : 32 * q + 12, :].bitcast(I32), dy_scales[2, 4 * q : 4 * q + 4, :].bitcast(I32))
+        for s in range(1, PASSES):
+            nc.sync.dma_start(dyw[s][:], dy_words[s].rearrange("p t d -> p (t d)").bitcast(I32))
+        nc.scalar.dma_start(gate_rows[:], gate.rearrange("p (e j) -> (p e) j", j=C)[0:P, :])
+
+        def load_scales(queue, planes, rows):
+            for r in range(4):
+                queue.dma_start(planes[r:P:32].bitcast(I32), rows[r].bitcast(I32))
+
+        def load_wbs(queue, lo, hi):
+            load_scales(
+                queue,
+                wbs[:, lo * PASSES : hi * PASSES, :],
+                wbt_scales[lo:hi].rearrange("e s (q r) i -> r q (e s) i", r=4),
+            )
+
+        def load_wb(e):
+            nc.sync.dma_start(wbw[e][:].bitcast(I32), wbt_words[e].rearrange("s p b -> p s b").bitcast(I32))
+
+        def load_a(g):
+            nc.sync.dma_start(a_sb[g][:], a.rearrange("(p t) j -> p t j", t=4)[:, :, 2 * C * g : 2 * C * (g + 1)])
+
+        load_wbs(nc.scalar, 0, 2)
+        load_wb(0)
+        load_a(0)
+        load_wb(1)
+        nc.sync.dma_start(waw[:].bitcast(I32), wat_words.rearrange("e s p b -> p (e s) b").bitcast(I32))
+        load_scales(nc.sync, was[:], wat_scales.rearrange("e s (q r) k -> r q (e s) k", r=4))
+        load_wbs(nc.sync, 2, E)
+        load_wb(2)
+        load_a(1)
+        load_wb(3)
+        load_wb(4)
+        load_a(2)
+        load_wb(5)
+        nc.sync.dma_start(wtw[:], wt_words.rearrange("s p k d -> p s (k d)").bitcast(I32))
+        load_scales(nc.sync, wts[:], wt_scales.rearrange("s (q r) k -> r q s k", r=4))
+
+        gate_ps = psum.tile([P, 2, C], F32, name="turned")
+        nc.tensor.transpose(gate_ps[:, 0, :], gate_rows[:], ident[:])
+        nc.scalar.activation(gate_col[:], gate_ps[:, 0, 0:8], ACT.Copy)
+
+        def gather_words(s, lo, hi):
+            nc.vector.tensor_copy(
+                gw[s][:, lo:hi].bitcast(U32), dyw[s][:].bitcast(U32).indirect(offsets[:, lo // 16 : hi // 16])
+            )
+
+        nc.vector.tensor_copy(gs[0][:], dys[:].indirect(offsets[:]))
+        for s in range(1, PASSES):
+            nc.scalar.dma_start(gs[s][0:100, :].bitcast(I32), gs[0][4 * s : 100 + 4 * s, :].bitcast(I32))
+        gather_words(0, 0, S)
+        gather_words(1, 0, 2 * C)
+        gather_words(2, 0, 2 * C)
+        gather_words(1, 2 * C, S)
+        gather_words(2, 2 * C, S)
+
+        mask, sums, gated, turned, dh, codes, code_scales, dx_ps = {}, {}, {}, {}, {}, {}, {}, {}
+
+        def make_mask(e):
+            sign = ring.tile([P, C, 4], BF16, name="sign")
+            nc.scalar.activation(
+                sign[:], a_sb[e // 2][:, :, (e % 2) * C : (e % 2 + 1) * C].rearrange("p t j -> p j t"), ACT.Sign
+            )
+            mask[e] = ring.tile([P, C * 4], BF16, name="mask")
+            nc.scalar.activation(mask[e][:], sign[:].rearrange("p j t -> p (j t)"), ACT.Relu)
+
+        def first_product(e):
+            cols = slice(e * C, (e + 1) * C)
+            sums[e] = psum.tile([P, H], F32, name="sums")
+            for s in range(PASSES):
+                nc.tensor.matmul_mx(
+                    out=sums[e][:],
+                    lhsT=gw[s][:, cols].bitcast(FP8X4),
+                    lhsT_scale=gs[s][:, cols],
+                    rhs=wbw[e][:, s, :].bitcast(FP4X4),
+                    rhs_scale=wbs[:, e * PASSES + s, :],
+                    start=(s == 0),
+                    stop=(s == PASSES - 1),
+                )
+
+        def apply_gate(e):
+            gated[e] = ring.tile([P, H], BF16, name="gated", align_bytes=64)
+            nc.scalar.activation(
+                gated[e][:].rearrange("j (u p c) -> j u p c", u=2, c=2),
+                sums[e][:].rearrange("j (p u c) -> j u p c", u=2, c=2),
+                ACT.Copy,
+                scale=gate_col[:, e : e + 1],
+            )
+
+        def turn(e):
+            turned[e] = psum.tile([P, 2, C], F32, name="turned")
+            for u in range(2):
+                nc.tensor.transpose(turned[e][:, u, :], gated[e][:].bitcast(F32)[:, u * P : (u + 1) * P], ident[:])
+
+        def apply_mask(e):
+            dh[e] = ring.tile([P, C * 4], BF16, name="dh", align_bytes=64)
+            nc.vector.tensor_tensor(
+                dh[e][:].rearrange("p (j u c) -> p j u c", u=2, c=2),
+                turned[e][:].bitcast(BF16).rearrange("p u (j c) -> p j u c", c=2),
+                mask[e][:].rearrange("p (j u c) -> p j u c", u=2, c=2),
+                ALU.mult,
+            )
+
+        def quantize(e):
+            codes[e] = ring.tile([P, C], U32, name="codes", align_bytes=64)
+            code_scales[e] = ring.tile([P, C], U8, name="code_scales", align_bytes=64)
+            nc.vector.quantize_mx(out=codes[e][:].bitcast(FP8X4), scales=code_scales[e][:], in_=dh[e][:])
+
+        def second_product(e):
+            dx_ps[e] = psum.tile([P, 2, C], F32, name="dx_ps")
+            for kt in range(2):
+                nc.tensor.matmul_mx(
+                    out=dx_ps[e][:, kt, :],
+                    lhsT=waw[:, e, 2 * P * kt : 2 * P * (kt + 1)].bitcast(FP4X4),
+                    lhsT_scale=was[:, e, P * kt : P * (kt + 1)],
+                    rhs=codes[e][:].bitcast(FP8X4),
+                    rhs_scale=code_scales[e][:],
+                    start=True,
+                    stop=True,
+                )
+
+        def copy_dx(e):
+            nc.scalar.activation(dx[:, :, e * C : (e + 1) * C], dx_ps[e][:], ACT.Copy)
+
+        def scatter(kt, e):
+            nc.vector.tensor_copy(
+                win[kt][:].indirect(offsets[:, e * C // 16 : (e + 1) * C // 16]), dx[:, kt, e * C : (e + 1) * C]
+            )
+
+        def base(kt, h, tag):
+            bank = psum.tile([P, 512], F32, name=tag)
+            cols = slice(512 * h, 512 * (h + 1))
+            for s in range(PASSES):
+                nc.tensor.matmul_mx(
+                    out=bank[:],
+                    lhsT=wtw[:, s, P * kt : P * (kt + 1)].bitcast(FP8X4),
+                    lhsT_scale=wts[:, s, P * kt : P * (kt + 1)],
+                    rhs=dyw[s][:, cols].bitcast(FP8X4),
+                    rhs_scale=dys[4 * s : P, cols],
+                    start=(s == 0),
+                    stop=(s == PASSES - 1),
+                )
+            return bank
+
+        def finish(kt, h, bank):
+            cols = slice(512 * h, 512 * (h + 1))
+            nc.vector.tensor_tensor(res[kt][:, cols], win[kt][:, cols], bank[:], ALU.add)
+            nc.sync.dma_start(out[P * kt : P * (kt + 1), cols], res[kt][:, cols])
+
+        make_mask(0)
+        first_product(0)
+        apply_gate(0)
+        first_product(1)
+        turn(0)
+        apply_gate(1)
+        make_mask(1)
+        turn(1)
+        for e in range(E):
+            apply_mask(e)
+            if e + 2 < E:
+                first_product(e + 2)
+                apply_gate(e + 2)
+            if e >= 2:
+                scatter(1, e - 2)
+            quantize(e)
+            second_product(e)
+            if e + 2 < E:
+                turn(e + 2)
+            if e >= 1:
+                scatter(0, e - 1)
+            copy_dx(e)
+            if e + 2 < E:
+                make_mask(e + 2)
+        banks0 = [base(0, h, "sums") for h in range(2)]
+        banks1 = [base(1, h, "turned") for h in range(2)]
+        scatter(0, E - 1)
+        scatter(1, E - 2)
+        for h in range(2):
+            finish(0, h, banks0[h])
+        scatter(1, E - 1)
+        for h in range(2):
+            finish(1, h, banks1[h])

@@ -28,23 +28,23 @@ def tile_moe_adb_relu_kernel(
     with ExitStack() as ctx:
         keep = ctx.enter_context(tc.tile_pool(name="keep", bufs=1))
         ring = ctx.enter_context(tc.tile_pool(name="ring", bufs=3))
+        stream = ctx.enter_context(tc.tile_pool(name="stream", bufs=2))
         psum = ctx.enter_context(tc.psum_pool(name="psum", bufs=2))
 
         def held(shape, dtype, name):
             return keep.tile(shape, dtype, name=name, align_bytes=64)
 
         offsets = keep.tile([P, S // 16], U16, name="offsets")
-        dyw = [held([P, T], I32, "dyw%d" % s) for s in range(PASSES)]
-        dys = held([P, T], U8, "dys")
+        dyw_first = held([P, T], I32, "dyw_first")
+        dyw_rest = held([P, PASSES - 1, T], I32, "dyw_rest")
+        dyw = [dyw_first[:], dyw_rest[:, 0, :], dyw_rest[:, 1, :]]
+        dys = held([P, PASSES, T], U8, "dys")
         gw = [held([P, S], I32, "gw%d" % s) for s in range(PASSES)]
         gs = [held([P, S], U8, "gs%d" % s) for s in range(PASSES)]
-        wtw = held([P, PASSES, K], I32, "wtw")
         wts = held([P, PASSES, K], U8, "wts")
-        wbw = [held([P, PASSES, 2 * H], U8, "wbw%d" % e) for e in range(E)]
         wbs = held([P, E * PASSES, H], U8, "wbs")
-        waw = held([P, E, 2 * K], U8, "waw")
         was = held([P, E, K], U8, "was")
-        a_sb = [held([P, 4, 2 * C], F32, "a%d" % g) for g in range(E // 2)]
+        waw = held([P, E, 2 * K], U8, "waw")
         gate_rows = held([P, C], F32, "gate_rows")
         gate_col = held([P, 8], F32, "gate_col")
         ident = held([P, P], F32, "ident")
@@ -52,88 +52,93 @@ def tile_moe_adb_relu_kernel(
         win = [held([P, T], F32, "win%d" % kt) for kt in range(2)]
         res = [held([P, T], F32, "res%d" % kt) for kt in range(2)]
 
-        def zero(tile2d):
-            nc.vector.memset(tile2d.bitcast(I32), 0)
+        def zero(engine, planes):
+            engine.memset(planes.rearrange("p a b -> p (a b)").bitcast(I32), 0)
 
-        zero(dys[:])
-        zero(wbs[:].rearrange("p a b -> p (a b)"))
-        zero(gs[1][:])
-        zero(gs[2][:])
-        zero(was[:].rearrange("p a b -> p (a b)"))
-        zero(wts[:].rearrange("p a b -> p (a b)"))
-        make_identity(nc, ident[:])
-        for kt in range(2):
-            nc.gpsimd.memset(win[kt][:], 0.0)
-
-        nc.sync.dma_start(offsets[:], offs)
-        nc.sync.dma_start(dyw[0][:], dy_words[0].rearrange("p t d -> p (t d)").bitcast(I32))
-        for q in range(4):
-            nc.scalar.dma_start(dys[32 * q : 32 * q + 8, :].bitcast(I32), dy_scales[0:2, 4 * q : 4 * q + 4, :].bitcast(I32))
-            nc.scalar.dma_start(dys[32 * q + 8 : 32 * q + 12, :].bitcast(I32), dy_scales[2, 4 * q : 4 * q + 4, :].bitcast(I32))
-        for s in range(1, PASSES):
-            nc.sync.dma_start(dyw[s][:], dy_words[s].rearrange("p t d -> p (t d)").bitcast(I32))
-        nc.scalar.dma_start(gate_rows[:], gate.rearrange("p (e j) -> (p e) j", j=C)[0:P, :])
+        zero(nc.gpsimd, dys[:])
+        zero(nc.vector, wbs[:, 0 : 2 * PASSES, :])
+        zero(nc.vector, was[:])
+        zero(nc.gpsimd, wbs[:, 2 * PASSES : 4 * PASSES, :])
+        zero(nc.vector, wbs[:, 4 * PASSES :, :])
+        zero(nc.vector, wts[:])
 
         def load_scales(queue, planes, rows):
             for r in range(4):
                 queue.dma_start(planes[r:P:32].bitcast(I32), rows[r].bitcast(I32))
 
-        def load_wbs(queue, lo, hi):
+        def load_wbs(lo, hi):
             load_scales(
-                queue,
+                nc.sync,
                 wbs[:, lo * PASSES : hi * PASSES, :],
                 wbt_scales[lo:hi].rearrange("e s (q r) i -> r q (e s) i", r=4),
             )
 
+        wbw, a_sb = {}, {}
+
         def load_wb(e):
+            wbw[e] = stream.tile([P, PASSES, 2 * H], U8, name="weights", align_bytes=64)
             nc.sync.dma_start(wbw[e][:].bitcast(I32), wbt_words[e].rearrange("s p b -> p s b").bitcast(I32))
 
-        def load_a(g):
+        def load_a(g, tag):
+            a_sb[g] = held([P, 4, 2 * C], F32, tag)
             nc.sync.dma_start(a_sb[g][:], a.rearrange("(p t) j -> p t j", t=4)[:, :, 2 * C * g : 2 * C * (g + 1)])
 
-        load_wbs(nc.scalar, 0, 2)
+        make_identity(nc, ident[:])
+        nc.sync.dma_start(offsets[:], offs)
+        nc.sync.dma_start(dyw_first[:], dy_words[0].rearrange("p t d -> p (t d)").bitcast(I32))
+        load_scales(nc.sync, dys[:], dy_scales.rearrange("s (q r) t -> r q s t", r=4))
+        nc.sync.dma_start(dyw_rest[:], dy_words[1:PASSES].rearrange("s p t d -> p s (t d)").bitcast(I32))
+        load_wbs(0, 2)
         load_wb(0)
-        load_a(0)
+        nc.sync.dma_start(gate_rows[:], gate.rearrange("p (e j) -> (p e) j", j=C)[0:P, :])
+        load_a(0, "a_pair")
         load_wb(1)
         nc.sync.dma_start(waw[:].bitcast(I32), wat_words.rearrange("e s p b -> p (e s) b").bitcast(I32))
         load_scales(nc.sync, was[:], wat_scales.rearrange("e s (q r) k -> r q (e s) k", r=4))
-        load_wbs(nc.sync, 2, E)
-        load_wb(2)
-        load_a(1)
-        load_wb(3)
-        load_wb(4)
-        load_a(2)
-        load_wb(5)
-        nc.sync.dma_start(wtw[:], wt_words.rearrange("s p k d -> p s (k d)").bitcast(I32))
+        load_wbs(2, 4)
+        load_wbs(4, E)
         load_scales(nc.sync, wts[:], wt_scales.rearrange("s (q r) k -> r q s k", r=4))
+        for kt in range(2):
+            nc.scalar.activation(
+                win[kt][:].rearrange("p (a b) -> p a b", b=P),
+                ident[:].unsqueeze(1).to_broadcast([P, T // P, P]),
+                ACT.Copy,
+                scale=0.0,
+            )
+
+        def gather_words(s, lo, hi):
+            nc.vector.tensor_copy(
+                gw[s][:, lo:hi].bitcast(U32), dyw[s].bitcast(U32).indirect(offsets[:, lo // 16 : hi // 16])
+            )
+
+        def gather_scales(s, lo, hi):
+            nc.vector.tensor_copy(gs[s][:, lo:hi], dys[:, s, :].indirect(offsets[:, lo // 16 : hi // 16]))
+
+        def gather_pair(g):
+            lo, hi = 2 * C * g, 2 * C * (g + 1)
+            for s in range(PASSES):
+                if s > 0:
+                    gather_words(s, lo, hi)
+                gather_scales(s, lo, hi)
 
         gate_ps = psum.tile([P, 2, C], F32, name="turned")
         nc.tensor.transpose(gate_ps[:, 0, :], gate_rows[:], ident[:])
         nc.scalar.activation(gate_col[:], gate_ps[:, 0, 0:8], ACT.Copy)
+        load_a(1, "gate_rows")
 
-        def gather_words(s, lo, hi):
-            nc.vector.tensor_copy(
-                gw[s][:, lo:hi].bitcast(U32), dyw[s][:].bitcast(U32).indirect(offsets[:, lo // 16 : hi // 16])
-            )
-
-        nc.vector.tensor_copy(gs[0][:], dys[:].indirect(offsets[:]))
-        for s in range(1, PASSES):
-            nc.scalar.dma_start(gs[s][0:100, :].bitcast(I32), gs[0][4 * s : 100 + 4 * s, :].bitcast(I32))
         gather_words(0, 0, S)
-        gather_words(1, 0, 2 * C)
-        gather_words(2, 0, 2 * C)
-        gather_words(1, 2 * C, S)
-        gather_words(2, 2 * C, S)
+        gather_pair(0)
 
         mask, sums, gated, turned, dh, codes, code_scales, dx_ps = {}, {}, {}, {}, {}, {}, {}, {}
 
         def make_mask(e):
-            sign = ring.tile([P, C, 4], BF16, name="sign")
+            mask[e] = stream.tile([P, C * 4], BF16, name="mask")
             nc.scalar.activation(
-                sign[:], a_sb[e // 2][:, :, (e % 2) * C : (e % 2 + 1) * C].rearrange("p t j -> p j t"), ACT.Sign
+                mask[e][:].rearrange("p (j t) -> p j t", t=4),
+                a_sb[e // 2][:, :, (e % 2) * C : (e % 2 + 1) * C].rearrange("p t j -> p j t"),
+                ACT.Sign,
             )
-            mask[e] = ring.tile([P, C * 4], BF16, name="mask")
-            nc.scalar.activation(mask[e][:], sign[:].rearrange("p j t -> p (j t)"), ACT.Relu)
+            nc.scalar.activation(mask[e][:], mask[e][:], ACT.Relu)
 
         def first_product(e):
             cols = slice(e * C, (e + 1) * C)
@@ -207,7 +212,7 @@ def tile_moe_adb_relu_kernel(
                     lhsT=wtw[:, s, P * kt : P * (kt + 1)].bitcast(FP8X4),
                     lhsT_scale=wts[:, s, P * kt : P * (kt + 1)],
                     rhs=dyw[s][:, cols].bitcast(FP8X4),
-                    rhs_scale=dys[4 * s : P, cols],
+                    rhs_scale=dys[:, s, cols],
                     start=(s == 0),
                     stop=(s == PASSES - 1),
                 )
@@ -225,10 +230,15 @@ def tile_moe_adb_relu_kernel(
         turn(0)
         apply_gate(1)
         make_mask(1)
+        load_a(2, "a_pair")
         turn(1)
+        gather_pair(1)
         for e in range(E):
             apply_mask(e)
+            if e == 2:
+                gather_pair(2)
             if e + 2 < E:
+                load_wb(e + 2)
                 first_product(e + 2)
                 apply_gate(e + 2)
             if e >= 2:
@@ -242,6 +252,8 @@ def tile_moe_adb_relu_kernel(
             copy_dx(e)
             if e + 2 < E:
                 make_mask(e + 2)
+        wtw = stream.tile([P, PASSES, K], I32, name="weights", align_bytes=64)
+        nc.sync.dma_start(wtw[:], wt_words.rearrange("s p k d -> p s (k d)").bitcast(I32))
         banks0 = [base(0, h, "sums") for h in range(2)]
         banks1 = [base(1, h, "turned") for h in range(2)]
         scatter(0, E - 1)

@@ -35,40 +35,40 @@ def tile_moe_adb_relu_kernel(
             return keep.tile(shape, dtype, name=name, align_bytes=64)
 
         offsets = keep.tile([P, S // 16], U16, name="offsets")
-        dyw_first = held([P, T], I32, "dyw_first")
-        dyw_rest = held([P, PASSES - 1, T], I32, "dyw_rest")
-        dyw = [dyw_first[:], dyw_rest[:, 0, :], dyw_rest[:, 1, :]]
+        dyw = [held([P, T], I32, "dyw%d" % s) for s in range(PASSES)]
         dys = held([P, PASSES, T], U8, "dys")
         gw = [held([P, S], I32, "gw%d" % s) for s in range(PASSES)]
         gs = [held([P, S], U8, "gs%d" % s) for s in range(PASSES)]
         wts = held([P, PASSES, K], U8, "wts")
         wbs = held([P, E * PASSES, H], U8, "wbs")
         was = held([P, E, K], U8, "was")
-        waw = held([P, E, 2 * K], U8, "waw")
-        gate_rows = held([P, C], F32, "gate_rows")
+        gate_rows = stream.tile([P, C], F32, name="a_pair", align_bytes=64)
+        zeros = [stream.tile([P, P], F32, name="weights", align_bytes=64), held([P, P], F32, "waw")]
         gate_col = held([P, 8], F32, "gate_col")
         ident = held([P, P], F32, "ident")
         dx = held([P, 2, S], F32, "dx")
         win = [held([P, T], F32, "win%d" % kt) for kt in range(2)]
         res = [held([P, T], F32, "res%d" % kt) for kt in range(2)]
 
-        def zero(engine, planes):
-            engine.memset(planes.rearrange("p a b -> p (a b)").bitcast(I32), 0)
+        def zero(planes):
+            nc.vector.memset(planes.rearrange("p a b -> p (a b)").bitcast(I32), 0)
 
-        zero(nc.gpsimd, dys[:])
-        zero(nc.vector, wbs[:, 0 : 2 * PASSES, :])
-        zero(nc.vector, was[:])
-        zero(nc.gpsimd, wbs[:, 2 * PASSES : 4 * PASSES, :])
-        zero(nc.vector, wbs[:, 4 * PASSES :, :])
-        zero(nc.vector, wts[:])
+        zero(wbs[:, 0 : 2 * PASSES, :])
+        zero(dys[:])
+        zero(was[:])
+        zero(wbs[:, 2 * PASSES :, :])
+        zero(wts[:])
+        for kt in range(2):
+            nc.gpsimd.memset(zeros[kt][:], 0.0)
+        make_identity(nc, ident[:])
 
         def load_scales(queue, planes, rows):
             for r in range(4):
                 queue.dma_start(planes[r:P:32].bitcast(I32), rows[r].bitcast(I32))
 
-        def load_wbs(lo, hi):
+        def load_wbs(queue, lo, hi):
             load_scales(
-                nc.sync,
+                queue,
                 wbs[:, lo * PASSES : hi * PASSES, :],
                 wbt_scales[lo:hi].rearrange("e s (q r) i -> r q (e s) i", r=4),
             )
@@ -79,54 +79,50 @@ def tile_moe_adb_relu_kernel(
             wbw[e] = stream.tile([P, PASSES, 2 * H], U8, name="weights", align_bytes=64)
             nc.sync.dma_start(wbw[e][:].bitcast(I32), wbt_words[e].rearrange("s p b -> p s b").bitcast(I32))
 
-        def load_a(g, tag):
-            a_sb[g] = held([P, 4, 2 * C], F32, tag)
+        def load_a(g):
+            a_sb[g] = stream.tile([P, 4, 2 * C], F32, name="a_pair", align_bytes=64)
             nc.sync.dma_start(a_sb[g][:], a.rearrange("(p t) j -> p t j", t=4)[:, :, 2 * C * g : 2 * C * (g + 1)])
 
-        make_identity(nc, ident[:])
         nc.sync.dma_start(offsets[:], offs)
-        nc.sync.dma_start(dyw_first[:], dy_words[0].rearrange("p t d -> p (t d)").bitcast(I32))
-        load_scales(nc.sync, dys[:], dy_scales.rearrange("s (q r) t -> r q s t", r=4))
-        nc.sync.dma_start(dyw_rest[:], dy_words[1:PASSES].rearrange("s p t d -> p s (t d)").bitcast(I32))
-        load_wbs(0, 2)
-        load_wb(0)
+        for s in range(PASSES):
+            nc.sync.dma_start(dyw[s][:], dy_words[s].rearrange("p t d -> p (t d)").bitcast(I32))
         nc.sync.dma_start(gate_rows[:], gate.rearrange("p (e j) -> (p e) j", j=C)[0:P, :])
-        load_a(0, "a_pair")
-        load_wb(1)
-        nc.sync.dma_start(waw[:].bitcast(I32), wat_words.rearrange("e s p b -> p (e s) b").bitcast(I32))
-        load_scales(nc.sync, was[:], wat_scales.rearrange("e s (q r) k -> r q (e s) k", r=4))
-        load_wbs(2, 4)
-        load_wbs(4, E)
-        load_scales(nc.sync, wts[:], wt_scales.rearrange("s (q r) k -> r q s k", r=4))
+        load_wb(0)
+        load_a(0)
+        load_scales(nc.sync, dys[:], dy_scales.rearrange("s (q r) t -> r q s t", r=4))
+        load_wbs(nc.sync, 2, E)
+        load_wbs(nc.gpsimd, 0, 2)
+        load_scales(nc.gpsimd, was[:], wat_scales.rearrange("e s (q r) k -> r q (e s) k", r=4))
+        load_scales(nc.gpsimd, wts[:], wt_scales.rearrange("s (q r) k -> r q s k", r=4))
         for kt in range(2):
             nc.scalar.activation(
                 win[kt][:].rearrange("p (a b) -> p a b", b=P),
-                ident[:].unsqueeze(1).to_broadcast([P, T // P, P]),
+                zeros[kt][:].unsqueeze(1).to_broadcast([P, T // P, P]),
                 ACT.Copy,
-                scale=0.0,
             )
+        load_wb(1)
+        waw = held([P, E, 2 * K], U8, "waw")
+        nc.sync.dma_start(waw[:].bitcast(I32), wat_words.rearrange("e s p b -> p (e s) b").bitcast(I32))
 
         def gather_words(s, lo, hi):
             nc.vector.tensor_copy(
-                gw[s][:, lo:hi].bitcast(U32), dyw[s].bitcast(U32).indirect(offsets[:, lo // 16 : hi // 16])
+                gw[s][:, lo:hi].bitcast(U32), dyw[s][:].bitcast(U32).indirect(offsets[:, lo // 16 : hi // 16])
             )
 
         def gather_scales(s, lo, hi):
             nc.vector.tensor_copy(gs[s][:, lo:hi], dys[:, s, :].indirect(offsets[:, lo // 16 : hi // 16]))
 
         def gather_pair(g):
-            lo, hi = 2 * C * g, 2 * C * (g + 1)
             for s in range(PASSES):
-                if s > 0:
-                    gather_words(s, lo, hi)
-                gather_scales(s, lo, hi)
+                gather_scales(s, 2 * C * g, 2 * C * (g + 1))
 
         gate_ps = psum.tile([P, 2, C], F32, name="turned")
         nc.tensor.transpose(gate_ps[:, 0, :], gate_rows[:], ident[:])
         nc.scalar.activation(gate_col[:], gate_ps[:, 0, 0:8], ACT.Copy)
-        load_a(1, "gate_rows")
+        load_a(1)
 
-        gather_words(0, 0, S)
+        for s in range(PASSES):
+            gather_words(s, 0, S)
         gather_pair(0)
 
         mask, sums, gated, turned, dh, codes, code_scales, dx_ps = {}, {}, {}, {}, {}, {}, {}, {}
@@ -230,7 +226,7 @@ def tile_moe_adb_relu_kernel(
         turn(0)
         apply_gate(1)
         make_mask(1)
-        load_a(2, "a_pair")
+        load_a(2)
         turn(1)
         gather_pair(1)
         for e in range(E):

@@ -1,7 +1,6 @@
 from contextlib import ExitStack
 
 import concourse.mybir as mybir
-from concourse.masks import make_identity
 
 K, T, E, C, H, N = 256, 1024, 6, 128, 512, 1536
 S = E * C
@@ -27,82 +26,97 @@ def tile_moe_adb_relu_kernel(
     nc = tc.nc
     with ExitStack() as ctx:
         keep = ctx.enter_context(tc.tile_pool(name="keep", bufs=1))
+        flow = ctx.enter_context(tc.tile_pool(name="flow", bufs=1))
         ring = ctx.enter_context(tc.tile_pool(name="ring", bufs=3))
-        stream = ctx.enter_context(tc.tile_pool(name="stream", bufs=2))
-        psum = ctx.enter_context(tc.psum_pool(name="psum", bufs=2))
+        psum = ctx.enter_context(tc.psum_pool(name="psum", bufs=1))
 
         def held(shape, dtype, name):
             return keep.tile(shape, dtype, name=name, align_bytes=64)
+
+        def placed(shape, dtype, name, offset):
+            return flow.tile(shape, dtype, name=name, align_bytes=64, offset=offset)
+
+        WB = PASSES * 2 * H
+        AB = 4 * 2 * C * 4
+        at_waw = 3 * WB + AB
+        at_was = at_waw + E * 2 * K
+        at_gate = at_was + E * K
+        at_wb = [0, WB, 2 * WB] + [at_gate + WB * n for n in range(3)]
+        at_a = [3 * WB] + [at_gate + 3 * WB + AB * n for n in range(2)]
+        flow_end = at_a[2] + AB
+        at_gated = [flow_end + 6 * H * n for n in range(2)]
+        at_mask = [at_gated[1 - n] + 3 * H for n in range(2)]
 
         offsets = keep.tile([P, S // 16], U16, name="offsets")
         dyw = [held([P, T], I32, "dyw%d" % s) for s in range(PASSES)]
         dys = held([P, PASSES, T], U8, "dys")
         gw = [held([P, S], I32, "gw%d" % s) for s in range(PASSES)]
         gs = [held([P, S], U8, "gs%d" % s) for s in range(PASSES)]
-        wts = held([P, PASSES, K], U8, "wts")
         wbs = held([P, E * PASSES, H], U8, "wbs")
-        was = held([P, E, K], U8, "was")
-        gate_rows = stream.tile([P, C], F32, name="a_pair", align_bytes=64)
-        zeros = [stream.tile([P, P], F32, name="weights", align_bytes=64), held([P, P], F32, "waw")]
+        blank = placed([P, (at_gate - WB) // 4], F32, "blank", WB)
         gate_col = held([P, 8], F32, "gate_col")
         ident = held([P, P], F32, "ident")
-        dx = held([P, 2, S], F32, "dx")
-        win = [held([P, T], F32, "win%d" % kt) for kt in range(2)]
         res = [held([P, T], F32, "res%d" % kt) for kt in range(2)]
 
         def zero(planes):
             nc.vector.memset(planes.rearrange("p a b -> p (a b)").bitcast(I32), 0)
 
-        zero(wbs[:, 0 : 2 * PASSES, :])
+        nc.gpsimd.memset(wbs[:, 3 * PASSES :, :].rearrange("p a b -> p (a b)").bitcast(I32), 0)
         zero(dys[:])
+        zero(wbs[:, 0 : 3 * PASSES, :])
+        nc.vector.memset(blank[:, 0:P], 0.0)
+        nc.gpsimd.affine_select(
+            out=ident[:],
+            in_=blank[:, 0:P],
+            compare_op=ALU.not_equal,
+            fill=1.0,
+            base=0,
+            pattern=[[-1, P]],
+            channel_multiplier=1,
+        )
+        was = placed([P, E, K], U8, "was", at_was)
         zero(was[:])
-        zero(wbs[:, 2 * PASSES :, :])
-        zero(wts[:])
-        for kt in range(2):
-            nc.gpsimd.memset(zeros[kt][:], 0.0)
-        make_identity(nc, ident[:])
 
         def load_scales(queue, planes, rows):
             for r in range(4):
                 queue.dma_start(planes[r:P:32].bitcast(I32), rows[r].bitcast(I32))
 
-        def load_wbs(queue, lo, hi):
-            load_scales(
-                queue,
-                wbs[:, lo * PASSES : hi * PASSES, :],
-                wbt_scales[lo:hi].rearrange("e s (q r) i -> r q (e s) i", r=4),
-            )
-
         wbw, a_sb = {}, {}
 
         def load_wb(e):
-            wbw[e] = stream.tile([P, PASSES, 2 * H], U8, name="weights", align_bytes=64)
+            wbw[e] = placed([P, PASSES, 2 * H], U8, "wbw%d" % e, at_wb[e])
             nc.sync.dma_start(wbw[e][:].bitcast(I32), wbt_words[e].rearrange("s p b -> p s b").bitcast(I32))
 
         def load_a(g):
-            a_sb[g] = stream.tile([P, 4, 2 * C], F32, name="a_pair", align_bytes=64)
+            a_sb[g] = placed([P, 4, 2 * C], F32, "a%d" % g, at_a[g])
             nc.sync.dma_start(a_sb[g][:], a.rearrange("(p t) j -> p t j", t=4)[:, :, 2 * C * g : 2 * C * (g + 1)])
 
         nc.sync.dma_start(offsets[:], offs)
         for s in range(PASSES):
             nc.sync.dma_start(dyw[s][:], dy_words[s].rearrange("p t d -> p (t d)").bitcast(I32))
-        nc.sync.dma_start(gate_rows[:], gate.rearrange("p (e j) -> (p e) j", j=C)[0:P, :])
+        gate_rows = placed([P, (flow_end - at_gate) // 4], F32, "gate_rows", at_gate)
+        nc.sync.dma_start(gate_rows[:, 0:C], gate.rearrange("p (e j) -> (p e) j", j=C)[0:P, :])
         load_wb(0)
-        load_a(0)
         load_scales(nc.sync, dys[:], dy_scales.rearrange("s (q r) t -> r q s t", r=4))
-        load_wbs(nc.sync, 2, E)
-        load_wbs(nc.gpsimd, 0, 2)
-        load_scales(nc.gpsimd, was[:], wat_scales.rearrange("e s (q r) k -> r q (e s) k", r=4))
-        load_scales(nc.gpsimd, wts[:], wt_scales.rearrange("s (q r) k -> r q s k", r=4))
-        for kt in range(2):
-            nc.scalar.activation(
-                win[kt][:].rearrange("p (a b) -> p a b", b=P),
-                zeros[kt][:].unsqueeze(1).to_broadcast([P, T // P, P]),
-                ACT.Copy,
-            )
+        load_scales(nc.sync, wbs[:], wbt_scales.rearrange("e s (q r) i -> r q (e s) i", r=4))
+        load_a(0)
         load_wb(1)
-        waw = held([P, E, 2 * K], U8, "waw")
+        load_wb(2)
+        waw = placed([P, E, 2 * K], U8, "waw", at_waw)
         nc.sync.dma_start(waw[:].bitcast(I32), wat_words.rearrange("e s p b -> p (e s) b").bitcast(I32))
+        load_scales(nc.sync, was[:], wat_scales.rearrange("e s (q r) k -> r q (e s) k", r=4))
+
+        def clear(window):
+            nc.scalar.activation(
+                window[:].rearrange("p (a b) -> p a b", b=P),
+                ident[:].unsqueeze(1).to_broadcast([P, T // P, P]),
+                ACT.Copy,
+                scale=0.0,
+            )
+
+        win = [held([P, T], F32, "win%d" % kt) for kt in range(2)]
+        for kt in range(2):
+            clear(win[kt])
 
         def gather_words(s, lo, hi):
             nc.vector.tensor_copy(
@@ -112,23 +126,28 @@ def tile_moe_adb_relu_kernel(
         def gather_scales(s, lo, hi):
             nc.vector.tensor_copy(gs[s][:, lo:hi], dys[:, s, :].indirect(offsets[:, lo // 16 : hi // 16]))
 
-        def gather_pair(g):
-            for s in range(PASSES):
-                gather_scales(s, 2 * C * g, 2 * C * (g + 1))
+        def bank_of(e, shape):
+            return psum.tile(shape, F32, name="bank%d" % (e % 3))
 
         gate_ps = psum.tile([P, 2, C], F32, name="turned")
-        nc.tensor.transpose(gate_ps[:, 0, :], gate_rows[:], ident[:])
+        nc.tensor.transpose(gate_ps[:, 0, :], gate_rows[:, 0:C], ident[:])
         nc.scalar.activation(gate_col[:], gate_ps[:, 0, 0:8], ACT.Copy)
         load_a(1)
+        load_wb(3)
+        load_wb(4)
+        load_a(2)
+        load_wb(5)
 
         for s in range(PASSES):
             gather_words(s, 0, S)
-        gather_pair(0)
+        for lo, hi in ((0, 2 * C), (2 * C, S)):
+            for s in range(PASSES):
+                gather_scales(s, lo, hi)
 
-        mask, sums, gated, turned, dh, codes, code_scales, dx_ps = {}, {}, {}, {}, {}, {}, {}, {}
+        mask, sums, gated, turned, dh, codes, code_scales, dx_ps, dx = {}, {}, {}, {}, {}, {}, {}, {}, {}
 
         def make_mask(e):
-            mask[e] = stream.tile([P, C * 4], BF16, name="mask")
+            mask[e] = placed([P, C * 4], BF16, "mask%d" % e, at_mask[e % 2])
             nc.scalar.activation(
                 mask[e][:].rearrange("p (j t) -> p j t", t=4),
                 a_sb[e // 2][:, :, (e % 2) * C : (e % 2 + 1) * C].rearrange("p t j -> p j t"),
@@ -138,7 +157,7 @@ def tile_moe_adb_relu_kernel(
 
         def first_product(e):
             cols = slice(e * C, (e + 1) * C)
-            sums[e] = psum.tile([P, H], F32, name="sums")
+            sums[e] = bank_of(e, [P, H])
             for s in range(PASSES):
                 nc.tensor.matmul_mx(
                     out=sums[e][:],
@@ -151,16 +170,16 @@ def tile_moe_adb_relu_kernel(
                 )
 
         def apply_gate(e):
-            gated[e] = ring.tile([P, H], BF16, name="gated", align_bytes=64)
+            gated[e] = placed([P, H + 2 * C + (32 if e == 0 else 0)], BF16, "gated%d" % e, at_gated[e % 2])
             nc.scalar.activation(
-                gated[e][:].rearrange("j (u p c) -> j u p c", u=2, c=2),
+                gated[e][:, 0:H].rearrange("j (u p c) -> j u p c", u=2, c=2),
                 sums[e][:].rearrange("j (p u c) -> j u p c", u=2, c=2),
                 ACT.Copy,
                 scale=gate_col[:, e : e + 1],
             )
 
         def turn(e):
-            turned[e] = psum.tile([P, 2, C], F32, name="turned")
+            turned[e] = bank_of(2, [P, 2, C]) if e == 0 else psum.tile([P, 2, C], F32, name="turned")
             for u in range(2):
                 nc.tensor.transpose(turned[e][:, u, :], gated[e][:].bitcast(F32)[:, u * P : (u + 1) * P], ident[:])
 
@@ -174,12 +193,15 @@ def tile_moe_adb_relu_kernel(
             )
 
         def quantize(e):
-            codes[e] = ring.tile([P, C], U32, name="codes", align_bytes=64)
-            code_scales[e] = ring.tile([P, C], U8, name="code_scales", align_bytes=64)
+            codes[e] = placed([P, C], U32, "codes%d" % e, at_gated[e % 2] + 2 * H)
+            if e == 0:
+                code_scales[e] = placed([P, C], U8, "code_scales0", at_mask[0])
+            else:
+                code_scales[e] = ring.tile([P, C], U8, name="code_scales", align_bytes=64)
             nc.vector.quantize_mx(out=codes[e][:].bitcast(FP8X4), scales=code_scales[e][:], in_=dh[e][:])
 
         def second_product(e):
-            dx_ps[e] = psum.tile([P, 2, C], F32, name="dx_ps")
+            dx_ps[e] = bank_of(e, [P, 2, C])
             for kt in range(2):
                 nc.tensor.matmul_mx(
                     out=dx_ps[e][:, kt, :],
@@ -192,15 +214,14 @@ def tile_moe_adb_relu_kernel(
                 )
 
         def copy_dx(e):
-            nc.scalar.activation(dx[:, :, e * C : (e + 1) * C], dx_ps[e][:], ACT.Copy)
+            dx[e] = placed([P, 2, C], F32, "dx%d" % e, at_gated[(e + 1) % 2])
+            nc.scalar.activation(dx[e][:], dx_ps[e][:], ACT.Copy)
 
         def scatter(kt, e):
-            nc.vector.tensor_copy(
-                win[kt][:].indirect(offsets[:, e * C // 16 : (e + 1) * C // 16]), dx[:, kt, e * C : (e + 1) * C]
-            )
+            nc.vector.tensor_copy(win[kt][:].indirect(offsets[:, e * C // 16 : (e + 1) * C // 16]), dx[e][:, kt, :])
 
-        def base(kt, h, tag):
-            bank = psum.tile([P, 512], F32, name=tag)
+        def base(kt, h):
+            bank = psum.tile([P, 512], F32, name="base%d%d" % (kt, h))
             cols = slice(512 * h, 512 * (h + 1))
             for s in range(PASSES):
                 nc.tensor.matmul_mx(
@@ -219,43 +240,36 @@ def tile_moe_adb_relu_kernel(
             nc.vector.tensor_tensor(res[kt][:, cols], win[kt][:, cols], bank[:], ALU.add)
             nc.sync.dma_start(out[P * kt : P * (kt + 1), cols], res[kt][:, cols])
 
-        make_mask(0)
-        first_product(0)
-        apply_gate(0)
-        first_product(1)
-        turn(0)
-        apply_gate(1)
-        make_mask(1)
-        load_a(2)
-        turn(1)
-        gather_pair(1)
-        for e in range(E):
-            apply_mask(e)
-            if e == 2:
-                gather_pair(2)
-            if e + 2 < E:
-                load_wb(e + 2)
-                first_product(e + 2)
-                apply_gate(e + 2)
-            if e >= 2:
-                scatter(1, e - 2)
-            quantize(e)
-            second_product(e)
-            if e + 2 < E:
-                turn(e + 2)
+        for e in range(2):
+            make_mask(e)
+            first_product(e)
+            apply_gate(e)
+            turn(e)
+        for e in range(E + 1):
+            if e < E:
+                apply_mask(e)
             if e >= 1:
                 scatter(0, e - 1)
-            copy_dx(e)
+            if e < E:
+                quantize(e)
+            if e >= 1:
+                scatter(1, e - 1)
+            if 1 <= e < E - 1:
+                turn(e + 1)
+            if e < E:
+                second_product(e)
+                if e + 2 < E:
+                    first_product(e + 2)
+                copy_dx(e)
             if e + 2 < E:
+                apply_gate(e + 2)
                 make_mask(e + 2)
-        wtw = stream.tile([P, PASSES, K], I32, name="weights", align_bytes=64)
+        wts = placed([P, PASSES, K], U8, "wts", at_wb[0])
+        zero(wts[:])
+        load_scales(nc.sync, wts[:], wt_scales.rearrange("s (q r) k -> r q s k", r=4))
+        wtw = placed([P, PASSES, K], I32, "wtw", at_wb[4])
         nc.sync.dma_start(wtw[:], wt_words.rearrange("s p k d -> p s (k d)").bitcast(I32))
-        banks0 = [base(0, h, "sums") for h in range(2)]
-        banks1 = [base(1, h, "turned") for h in range(2)]
-        scatter(0, E - 1)
-        scatter(1, E - 2)
-        for h in range(2):
-            finish(0, h, banks0[h])
-        scatter(1, E - 1)
-        for h in range(2):
-            finish(1, h, banks1[h])
+        banks = [[base(kt, h) for h in range(2)] for kt in range(2)]
+        for kt in range(2):
+            for h in range(2):
+                finish(kt, h, banks[kt][h])

@@ -1,6 +1,7 @@
 from contextlib import ExitStack
 
 import concourse.mybir as mybir
+from concourse.masks import make_identity
 
 K, T, E, C, H, N = 256, 1024, 6, 128, 512, 1536
 S = E * C
@@ -36,15 +37,7 @@ def tile_moe_adb_relu_kernel(
         def placed(shape, dtype, name, offset):
             return flow.tile(shape, dtype, name=name, align_bytes=64, offset=offset)
 
-        WB = PASSES * 2 * H
-        AB = 4 * 2 * C * 4
-        at_waw = 3 * WB + AB
-        at_was = at_waw + E * 2 * K
-        at_gate = at_was + E * K
-        at_wb = [0, WB, 2 * WB] + [at_gate + WB * n for n in range(3)]
-        at_a = [3 * WB] + [at_gate + 3 * WB + AB * n for n in range(2)]
-        flow_end = at_a[2] + AB
-        at_gated = [flow_end + 6 * H * n for n in range(2)]
+        at_gated = [6 * H * n for n in range(2)]
         at_mask = [at_gated[1 - n] + 3 * H for n in range(2)]
 
         offsets = keep.tile([P, S // 16], U16, name="offsets")
@@ -52,8 +45,9 @@ def tile_moe_adb_relu_kernel(
         dys = held([P, PASSES, T], U8, "dys")
         gw = [held([P, S], I32, "gw%d" % s) for s in range(PASSES)]
         gs = [held([P, S], U8, "gs%d" % s) for s in range(PASSES)]
-        wbs = held([P, E * PASSES, H], U8, "wbs")
-        blank = placed([P, (at_gate - WB) // 4], F32, "blank", WB)
+        wbs = [held([P, 3 * PASSES, H], U8, "wbs%d" % n) for n in range(2)]
+        was = held([P, E, K], U8, "was")
+        wts = held([P, PASSES, K], U8, "wts")
         gate_col = held([P, 8], F32, "gate_col")
         ident = held([P, P], F32, "ident")
         res = [held([P, T], F32, "res%d" % kt) for kt in range(2)]
@@ -61,21 +55,11 @@ def tile_moe_adb_relu_kernel(
         def zero(planes):
             nc.vector.memset(planes.rearrange("p a b -> p (a b)").bitcast(I32), 0)
 
-        nc.gpsimd.memset(wbs[:, 3 * PASSES :, :].rearrange("p a b -> p (a b)").bitcast(I32), 0)
-        zero(dys[:])
-        zero(wbs[:, 0 : 3 * PASSES, :])
-        nc.vector.memset(blank[:, 0:P], 0.0)
-        nc.gpsimd.affine_select(
-            out=ident[:],
-            in_=blank[:, 0:P],
-            compare_op=ALU.not_equal,
-            fill=1.0,
-            base=0,
-            pattern=[[-1, P]],
-            channel_multiplier=1,
-        )
-        was = placed([P, E, K], U8, "was", at_was)
-        zero(was[:])
+        for planes in (dys, wbs[0], was):
+            zero(planes[:])
+        for planes in (wbs[1], wts):
+            nc.gpsimd.memset(planes[:].rearrange("p a b -> p (a b)").bitcast(I32), 0)
+        make_identity(nc, ident[:])
 
         def load_scales(queue, planes, rows):
             for r in range(4):
@@ -84,39 +68,47 @@ def tile_moe_adb_relu_kernel(
         wbw, a_sb = {}, {}
 
         def load_wb(e):
-            wbw[e] = placed([P, PASSES, 2 * H], U8, "wbw%d" % e, at_wb[e])
+            wbw[e] = held([P, PASSES, 2 * H], U8, "wbw%d" % e)
             nc.sync.dma_start(wbw[e][:].bitcast(I32), wbt_words[e].rearrange("s p b -> p s b").bitcast(I32))
 
         def load_a(g):
-            a_sb[g] = placed([P, 4, 2 * C], F32, "a%d" % g, at_a[g])
+            a_sb[g] = held([P, 4, 2 * C], F32, "a%d" % g) if g else placed([P, 4, 2 * C], F32, "a0", 12 * H)
             nc.sync.dma_start(a_sb[g][:], a.rearrange("(p t) j -> p t j", t=4)[:, :, 2 * C * g : 2 * C * (g + 1)])
 
         nc.sync.dma_start(offsets[:], offs)
+        wb_rows = wbt_scales.rearrange("e s (q r) i -> r q (e s) i", r=4)
         for s in range(PASSES):
+            if s == PASSES - 1:
+                load_a(0)
             nc.sync.dma_start(dyw[s][:], dy_words[s].rearrange("p t d -> p (t d)").bitcast(I32))
-        gate_rows = placed([P, (flow_end - at_gate) // 4], F32, "gate_rows", at_gate)
-        nc.sync.dma_start(gate_rows[:, 0:C], gate.rearrange("p (e j) -> (p e) j", j=C)[0:P, :])
-        load_wb(0)
         load_scales(nc.sync, dys[:], dy_scales.rearrange("s (q r) t -> r q s t", r=4))
-        load_scales(nc.sync, wbs[:], wbt_scales.rearrange("e s (q r) i -> r q (e s) i", r=4))
-        load_a(0)
+        load_scales(nc.sync, wbs[0][:], wb_rows[:, :, 0 : 3 * PASSES, :])
+        gate_rows = held([P, C], F32, "gate_rows")
+        nc.sync.dma_start(gate_rows[:], gate.rearrange("p (e j) -> (p e) j", j=C)[0:P, :])
+        load_wb(0)
         load_wb(1)
-        load_wb(2)
-        waw = placed([P, E, 2 * K], U8, "waw", at_waw)
+        waw = held([P, E, 2 * K], U8, "waw")
         nc.sync.dma_start(waw[:].bitcast(I32), wat_words.rearrange("e s p b -> p (e s) b").bitcast(I32))
         load_scales(nc.sync, was[:], wat_scales.rearrange("e s (q r) k -> r q (e s) k", r=4))
+        load_wb(2)
+        load_a(1)
+        load_wb(3)
+        load_wb(4)
+        load_a(2)
+        load_wb(5)
+        load_scales(nc.gpsimd, wts[:], wt_scales.rearrange("s (q r) k -> r q s k", r=4))
+        wtw = held([P, PASSES, K], I32, "wtw")
+        nc.sync.dma_start(wtw[:], wt_words.rearrange("s p k d -> p s (k d)").bitcast(I32))
 
         def clear(window):
             nc.scalar.activation(
                 window[:].rearrange("p (a b) -> p a b", b=P),
-                ident[:].unsqueeze(1).to_broadcast([P, T // P, P]),
+                wbs[1][:].rearrange("p a b -> p (a b)").bitcast(F32)[:, 0:P].unsqueeze(1).to_broadcast([P, T // P, P]),
                 ACT.Copy,
-                scale=0.0,
             )
 
-        win = [held([P, T], F32, "win%d" % kt) for kt in range(2)]
-        for kt in range(2):
-            clear(win[kt])
+        win = [held([P, T], F32, "win0")]
+        clear(win[0])
 
         def gather_words(s, lo, hi):
             nc.vector.tensor_copy(
@@ -132,11 +124,6 @@ def tile_moe_adb_relu_kernel(
         gate_ps = psum.tile([P, 2, C], F32, name="turned")
         nc.tensor.transpose(gate_ps[:, 0, :], gate_rows[:, 0:C], ident[:])
         nc.scalar.activation(gate_col[:], gate_ps[:, 0, 0:8], ACT.Copy)
-        load_a(1)
-        load_wb(3)
-        load_wb(4)
-        load_a(2)
-        load_wb(5)
 
         for s in range(PASSES):
             gather_words(s, 0, S)
@@ -164,13 +151,13 @@ def tile_moe_adb_relu_kernel(
                     lhsT=gw[s][:, cols].bitcast(FP8X4),
                     lhsT_scale=gs[s][:, cols],
                     rhs=wbw[e][:, s, :].bitcast(FP4X4),
-                    rhs_scale=wbs[:, e * PASSES + s, :],
+                    rhs_scale=wbs[e // 3][:, (e % 3) * PASSES + s, :],
                     start=(s == 0),
                     stop=(s == PASSES - 1),
                 )
 
         def apply_gate(e):
-            gated[e] = placed([P, H + 2 * C + (32 if e == 0 else 0)], BF16, "gated%d" % e, at_gated[e % 2])
+            gated[e] = placed([P, H + 2 * C], BF16, "gated%d" % e, at_gated[e % 2])
             nc.scalar.activation(
                 gated[e][:, 0:H].rearrange("j (u p c) -> j u p c", u=2, c=2),
                 sums[e][:].rearrange("j (p u c) -> j u p c", u=2, c=2),
@@ -181,15 +168,12 @@ def tile_moe_adb_relu_kernel(
         def turn(e):
             turned[e] = bank_of(2, [P, 2, C]) if e == 0 else psum.tile([P, 2, C], F32, name="turned")
             for u in range(2):
-                nc.tensor.transpose(turned[e][:, u, :], gated[e][:].bitcast(F32)[:, u * P : (u + 1) * P], ident[:])
+                nc.tensor.transpose(turned[e][:].rearrange("p u j -> p (u j)")[:, u : 2 * C : 2], gated[e][:].bitcast(F32)[:, u * P : (u + 1) * P], ident[:])
 
         def apply_mask(e):
             dh[e] = ring.tile([P, C * 4], BF16, name="dh", align_bytes=64)
             nc.vector.tensor_tensor(
-                dh[e][:].rearrange("p (j u c) -> p j u c", u=2, c=2),
-                turned[e][:].bitcast(BF16).rearrange("p u (j c) -> p j u c", c=2),
-                mask[e][:].rearrange("p (j u c) -> p j u c", u=2, c=2),
-                ALU.mult,
+                dh[e][:], turned[e][:].rearrange("p u j -> p (u j)").bitcast(BF16), mask[e][:], ALU.mult
             )
 
         def quantize(e):
@@ -235,13 +219,18 @@ def tile_moe_adb_relu_kernel(
                 )
             return bank
 
-        def finish(kt, h, bank):
-            cols = slice(512 * h, 512 * (h + 1))
-            nc.vector.tensor_tensor(res[kt][:, cols], win[kt][:, cols], bank[:], ALU.add)
-            nc.sync.dma_start(out[P * kt : P * (kt + 1), cols], res[kt][:, cols])
+        def finish(kt, lo, hi):
+            bank = banks[kt, lo // 512][:, lo % 512 : (hi - 1) % 512 + 1]
+            nc.vector.tensor_tensor(res[kt][:, lo:hi], win[kt][:, lo:hi], bank, ALU.add)
+            nc.sync.dma_start(out[P * kt : P * (kt + 1), lo:hi], res[kt][:, lo:hi])
 
         for e in range(2):
             make_mask(e)
+        win.append(placed([P, T], F32, "win1", 12 * H))
+        clear(win[1])
+        load_scales(nc.gpsimd, wbs[1][:], wb_rows[:, :, 3 * PASSES :, :])
+        banks = {}
+        for e in range(2):
             first_product(e)
             apply_gate(e)
             turn(e)
@@ -264,12 +253,7 @@ def tile_moe_adb_relu_kernel(
             if e + 2 < E:
                 apply_gate(e + 2)
                 make_mask(e + 2)
-        wts = placed([P, PASSES, K], U8, "wts", at_wb[0])
-        zero(wts[:])
-        load_scales(nc.sync, wts[:], wt_scales.rearrange("s (q r) k -> r q s k", r=4))
-        wtw = placed([P, PASSES, K], I32, "wtw", at_wb[4])
-        nc.sync.dma_start(wtw[:], wt_words.rearrange("s p k d -> p s (k d)").bitcast(I32))
-        banks = [[base(kt, h) for h in range(2)] for kt in range(2)]
-        for kt in range(2):
-            for h in range(2):
-                finish(kt, h, banks[kt][h])
+            if 2 <= e < E:
+                banks[divmod(e - 2, 2)] = base(*divmod(e - 2, 2))
+        for kt, lo, hi in ((0, 0, 512), (0, 512, T), (1, 0, 512), (1, 512, 768), (1, 768, T)):
+            finish(kt, lo, hi)

@@ -57,13 +57,15 @@ def tile_moe_adb_relu_kernel(
 
         for planes in (dys, wbs[0], was):
             zero(planes[:])
+        gate_rows = held([P, C], F32, "gate_rows")
+        nc.vector.memset(gate_rows[:], 0.0)
         for planes in (wbs[1], wts):
             nc.gpsimd.memset(planes[:].rearrange("p a b -> p (a b)").bitcast(I32), 0)
         make_identity(nc, ident[:])
 
-        def load_scales(queue, planes, rows):
+        def load_scales(queue, planes, rows, first=0):
             for r in range(4):
-                queue.dma_start(planes[r:P:32].bitcast(I32), rows[r].bitcast(I32))
+                queue.dma_start(planes[first + r : P : 32].bitcast(I32), rows[r].bitcast(I32))
 
         wbw, a_sb = {}, {}
 
@@ -83,8 +85,7 @@ def tile_moe_adb_relu_kernel(
             nc.sync.dma_start(dyw[s][:], dy_words[s].rearrange("p t d -> p (t d)").bitcast(I32))
         load_scales(nc.sync, dys[:], dy_scales.rearrange("s (q r) t -> r q s t", r=4))
         load_scales(nc.sync, wbs[0][:], wb_rows[:, :, 0 : 3 * PASSES, :])
-        gate_rows = held([P, C], F32, "gate_rows")
-        nc.sync.dma_start(gate_rows[:], gate.rearrange("p (e j) -> (p e) j", j=C)[0:P, :])
+        nc.sync.dma_start(gate_rows[0:8, :], gate.rearrange("p (e j) -> (p e) j", j=C)[0:8, :])
         load_wb(0)
         load_wb(1)
         waw = held([P, E, 2 * K], U8, "waw")
@@ -96,7 +97,7 @@ def tile_moe_adb_relu_kernel(
         load_wb(4)
         load_a(2)
         load_wb(5)
-        load_scales(nc.gpsimd, wts[:], wt_scales.rearrange("s (q r) k -> r q s k", r=4))
+        load_scales(nc.gpsimd, wts[:], wt_scales.rearrange("s (q r) k -> r q s k", r=4), 4)
         wtw = held([P, PASSES, K], I32, "wtw")
         nc.sync.dma_start(wtw[:], wt_words.rearrange("s p k d -> p s (k d)").bitcast(I32))
 
@@ -136,8 +137,8 @@ def tile_moe_adb_relu_kernel(
         def make_mask(e):
             mask[e] = placed([P, C * 4], BF16, "mask%d" % e, at_mask[e % 2])
             nc.scalar.activation(
-                mask[e][:].rearrange("p (j t) -> p j t", t=4),
-                a_sb[e // 2][:, :, (e % 2) * C : (e % 2 + 1) * C].rearrange("p t j -> p j t"),
+                mask[e][:].rearrange("p (c i t) -> p c t i", i=4, t=4),
+                a_sb[e // 2][:, :, (e % 2) * C : (e % 2 + 1) * C].rearrange("p t (c i) -> p c t i", i=4),
                 ACT.Sign,
             )
             nc.scalar.activation(mask[e][:], mask[e][:], ACT.Relu)
@@ -211,7 +212,7 @@ def tile_moe_adb_relu_kernel(
                 nc.tensor.matmul_mx(
                     out=bank[:],
                     lhsT=wtw[:, s, P * kt : P * (kt + 1)].bitcast(FP8X4),
-                    lhsT_scale=wts[:, s, P * kt : P * (kt + 1)],
+                    lhsT_scale=wts[4:P, s, P * kt : P * (kt + 1)],
                     rhs=dyw[s][:, cols].bitcast(FP8X4),
                     rhs_scale=dys[:, s, cols],
                     start=(s == 0),

@@ -48,7 +48,7 @@ def tile_moe_adb_relu_kernel(
         wbs = [held([P, 3 * PASSES, H], U8, "wbs%d" % n) for n in range(2)]
         was = held([P, E, K], U8, "was")
         wts = held([P, PASSES, K], U8, "wts")
-        gate_col = held([P, 8], F32, "gate_col")
+        gate_col = held([P, E], F32, "gate_col")
         ident = held([P, P], F32, "ident")
         res = [held([P, T], F32, "res%d" % kt) for kt in range(2)]
 
@@ -67,11 +67,16 @@ def tile_moe_adb_relu_kernel(
             for r in range(4):
                 queue.dma_start(planes[first + r : P : 32].bitcast(I32), rows[r].bitcast(I32))
 
-        wbw, a_sb = {}, {}
+        wbw, waw, a_sb = {}, {}, {}
 
         def load_wb(e):
             wbw[e] = held([P, PASSES, 2 * H], U8, "wbw%d" % e)
             nc.sync.dma_start(wbw[e][:].bitcast(I32), wbt_words[e].rearrange("s p b -> p s b").bitcast(I32))
+
+        def load_wa(g):
+            waw[g] = held([P, 3, 2 * K], U8, "waw%d" % g)
+            rows = wat_words[3 * g : 3 * (g + 1)].rearrange("e s p b -> p (e s) b")
+            nc.sync.dma_start(waw[g][:].bitcast(I32), rows.bitcast(I32))
 
         def load_a(g):
             a_sb[g] = held([P, 4, 2 * C], F32, "a%d" % g) if g else placed([P, 4, 2 * C], F32, "a0", 12 * H)
@@ -83,18 +88,18 @@ def tile_moe_adb_relu_kernel(
             if s == PASSES - 1:
                 load_a(0)
             nc.sync.dma_start(dyw[s][:], dy_words[s].rearrange("p t d -> p (t d)").bitcast(I32))
+        nc.sync.dma_start(gate_rows[0:E, :], gate.rearrange("p (e j) -> (p e) j", j=C)[0:E, :])
         load_scales(nc.sync, dys[:], dy_scales.rearrange("s (q r) t -> r q s t", r=4))
         load_scales(nc.sync, wbs[0][:], wb_rows[:, :, 0 : 3 * PASSES, :])
-        nc.sync.dma_start(gate_rows[0:8, :], gate.rearrange("p (e j) -> (p e) j", j=C)[0:8, :])
         load_wb(0)
         load_wb(1)
-        waw = held([P, E, 2 * K], U8, "waw")
-        nc.sync.dma_start(waw[:].bitcast(I32), wat_words.rearrange("e s p b -> p (e s) b").bitcast(I32))
-        load_scales(nc.sync, was[:], wat_scales.rearrange("e s (q r) k -> r q (e s) k", r=4))
+        load_wa(0)
         load_wb(2)
+        load_scales(nc.sync, was[:], wat_scales.rearrange("e s (q r) k -> r q (e s) k", r=4))
         load_a(1)
         load_wb(3)
         load_wb(4)
+        load_wa(1)
         load_a(2)
         load_wb(5)
         load_scales(nc.gpsimd, wts[:], wt_scales.rearrange("s (q r) k -> r q s k", r=4), 4)
@@ -124,7 +129,7 @@ def tile_moe_adb_relu_kernel(
 
         gate_ps = psum.tile([P, 2, C], F32, name="turned")
         nc.tensor.transpose(gate_ps[:, 0, :], gate_rows[:, 0:C], ident[:])
-        nc.scalar.activation(gate_col[:], gate_ps[:, 0, 0:8], ACT.Copy)
+        nc.scalar.activation(gate_col[:], gate_ps[:, 0, 0:E], ACT.Copy)
 
         for s in range(PASSES):
             gather_words(s, 0, S)
@@ -190,7 +195,7 @@ def tile_moe_adb_relu_kernel(
             for kt in range(2):
                 nc.tensor.matmul_mx(
                     out=dx_ps[e][:, kt, :],
-                    lhsT=waw[:, e, 2 * P * kt : 2 * P * (kt + 1)].bitcast(FP4X4),
+                    lhsT=waw[e // 3][:, e % 3, 2 * P * kt : 2 * P * (kt + 1)].bitcast(FP4X4),
                     lhsT_scale=was[:, e, P * kt : P * (kt + 1)],
                     rhs=codes[e][:].bitcast(FP8X4),
                     rhs_scale=code_scales[e][:],

@@ -37,15 +37,17 @@ def tile_moe_adb_relu_kernel(
         def placed(shape, dtype, name, offset):
             return flow.tile(shape, dtype, name=name, align_bytes=64, offset=offset)
 
-        at_gated = [6 * H * n for n in range(2)]
-        at_mask = [at_gated[1 - n] + 3 * H for n in range(2)]
+        at_wb = [6 * H * e for e in range(E)]
+        at_gated = [6 * H * E + 2 * H * e for e in range(E)]
+        at_mask = [6 * H * E + 2 * H * E + 2 * H * e for e in range(2)] + at_wb[2:]
+        at_sign = [6 * H * E + 2 * H * (E + 2) + 2 * H * e for e in range(2)] + [at + 2 * H for at in at_wb[1:]]
 
         offsets = keep.tile([P, S // 16], U16, name="offsets")
         dyw = [held([P, T], I32, "dyw%d" % s) for s in range(PASSES)]
         dys = held([P, PASSES, T], U8, "dys")
         gw = [held([P, S], I32, "gw%d" % s) for s in range(PASSES)]
-        gs = [held([P, S], U8, "gs%d" % s) for s in range(PASSES)]
-        wbs = [held([P, 3 * PASSES, H], U8, "wbs%d" % n) for n in range(2)]
+        gs = [held([P, 4 * C], U8, "gs%d" % s) for s in range(PASSES)]
+        wbs = [held([P, 2 * PASSES, H], U8, "wbs%d" % g) for g in range(3)]
         was = held([P, E, K], U8, "was")
         wts = held([P, PASSES, K], U8, "wts")
         gate_col = held([P, E], F32, "gate_col")
@@ -55,12 +57,14 @@ def tile_moe_adb_relu_kernel(
         def zero(planes):
             nc.vector.memset(planes.rearrange("p a b -> p (a b)").bitcast(I32), 0)
 
-        for planes in (dys, wbs[0], was):
+        for planes in (dys, wbs[0]):
             zero(planes[:])
         gate_rows = held([P, C], F32, "gate_rows")
         nc.vector.memset(gate_rows[:], 0.0)
-        for planes in (wbs[1], wts):
+        zeros = held([P, P], F32, "zeros")
+        for planes in (wts, wbs[1], was, wbs[2]):
             nc.gpsimd.memset(planes[:].rearrange("p a b -> p (a b)").bitcast(I32), 0)
+        nc.gpsimd.memset(zeros[:], 0.0)
         make_identity(nc, ident[:])
 
         def load_scales(queue, planes, rows, first=0):
@@ -70,7 +74,7 @@ def tile_moe_adb_relu_kernel(
         wbw, waw, a_sb = {}, {}, {}
 
         def load_wb(e):
-            wbw[e] = held([P, PASSES, 2 * H], U8, "wbw%d" % e)
+            wbw[e] = placed([P, PASSES, 2 * H], U8, "wbw%d" % e, at_wb[e])
             nc.sync.dma_start(wbw[e][:].bitcast(I32), wbt_words[e].rearrange("s p b -> p s b").bitcast(I32))
 
         def load_wa(g):
@@ -79,7 +83,7 @@ def tile_moe_adb_relu_kernel(
             nc.sync.dma_start(waw[g][:].bitcast(I32), rows.bitcast(I32))
 
         def load_a(g):
-            a_sb[g] = held([P, 4, 2 * C], F32, "a%d" % g) if g else placed([P, 4, 2 * C], F32, "a0", 12 * H)
+            a_sb[g] = held([P, 4, 2 * C], F32, "a%d" % g)
             nc.sync.dma_start(a_sb[g][:], a.rearrange("(p t) j -> p t j", t=4)[:, :, 2 * C * g : 2 * C * (g + 1)])
 
         nc.sync.dma_start(offsets[:], offs)
@@ -90,17 +94,23 @@ def tile_moe_adb_relu_kernel(
             nc.sync.dma_start(dyw[s][:], dy_words[s].rearrange("p t d -> p (t d)").bitcast(I32))
         nc.sync.dma_start(gate_rows[0:E, :], gate.rearrange("p (e j) -> (p e) j", j=C)[0:E, :])
         load_scales(nc.sync, dys[:], dy_scales.rearrange("s (q r) t -> r q s t", r=4))
-        load_scales(nc.sync, wbs[0][:], wb_rows[:, :, 0 : 3 * PASSES, :])
+
+        def load_wb_scales(g):
+            load_scales(nc.sync, wbs[g][:], wb_rows[:, :, 2 * PASSES * g : 2 * PASSES * (g + 1), :])
+
+        load_wb_scales(0)
         load_wb(0)
         load_wb(1)
         load_wa(0)
-        load_wb(2)
         load_scales(nc.sync, was[:], wat_scales.rearrange("e s (q r) k -> r q (e s) k", r=4))
         load_a(1)
+        load_wb_scales(1)
+        load_wb(2)
         load_wb(3)
-        load_wb(4)
         load_wa(1)
         load_a(2)
+        load_wb_scales(2)
+        load_wb(4)
         load_wb(5)
         load_scales(nc.gpsimd, wts[:], wt_scales.rearrange("s (q r) k -> r q s k", r=4), 4)
         wtw = held([P, PASSES, K], I32, "wtw")
@@ -109,20 +119,28 @@ def tile_moe_adb_relu_kernel(
         def clear(window):
             nc.scalar.activation(
                 window[:].rearrange("p (a b) -> p a b", b=P),
-                wbs[1][:].rearrange("p a b -> p (a b)").bitcast(F32)[:, 0:P].unsqueeze(1).to_broadcast([P, T // P, P]),
+                zeros[:].unsqueeze(1).to_broadcast([P, T // P, P]),
                 ACT.Copy,
             )
 
-        win = [held([P, T], F32, "win0")]
-        clear(win[0])
+        win = [held([P, T], F32, "win%d" % kt) for kt in range(2)]
+        for kt in range(2):
+            clear(win[kt])
 
         def gather_words(s, lo, hi):
             nc.vector.tensor_copy(
                 gw[s][:, lo:hi].bitcast(U32), dyw[s][:].bitcast(U32).indirect(offsets[:, lo // 16 : hi // 16])
             )
 
-        def gather_scales(s, lo, hi):
-            nc.vector.tensor_copy(gs[s][:, lo:hi], dys[:, s, :].indirect(offsets[:, lo // 16 : hi // 16]))
+        def gather_scales(dst, s, lo, hi):
+            nc.vector.tensor_copy(dst, dys[:, s, :].indirect(offsets[:, lo // 16 : hi // 16]))
+
+        late = {}
+
+        def gather_late(s):
+            at = (at_gated[0] + H, at_mask[0], at_gated[1] + H)[s]
+            late[s] = placed([P, 2 * C], U8, "late%d" % s, at)
+            gather_scales(late[s][:], s, 4 * C, S)
 
         def bank_of(e, shape):
             return psum.tile(shape, F32, name="bank%d" % (e % 3))
@@ -133,20 +151,23 @@ def tile_moe_adb_relu_kernel(
 
         for s in range(PASSES):
             gather_words(s, 0, S)
-        for lo, hi in ((0, 2 * C), (2 * C, S)):
+        for lo, hi in ((0, C), (C, 2 * C), (2 * C, 4 * C)):
             for s in range(PASSES):
-                gather_scales(s, lo, hi)
+                gather_scales(gs[s][:, lo:hi], s, lo, hi)
 
-        mask, sums, gated, turned, dh, codes, code_scales, dx_ps, dx = {}, {}, {}, {}, {}, {}, {}, {}, {}
+        sign, mask, sums, gated, turned, dh, codes, code_scales, dx_ps, dx = {}, {}, {}, {}, {}, {}, {}, {}, {}, {}
 
-        def make_mask(e):
-            mask[e] = placed([P, C * 4], BF16, "mask%d" % e, at_mask[e % 2])
+        def make_sign(e):
+            sign[e] = placed([P, C * 4], BF16, "sign%d" % e, at_sign[e])
             nc.scalar.activation(
-                mask[e][:].rearrange("p (c i t) -> p c t i", i=4, t=4),
+                sign[e][:].rearrange("p (c i t) -> p c t i", i=4, t=4),
                 a_sb[e // 2][:, :, (e % 2) * C : (e % 2 + 1) * C].rearrange("p t (c i) -> p c t i", i=4),
                 ACT.Sign,
             )
-            nc.scalar.activation(mask[e][:], mask[e][:], ACT.Relu)
+
+        def make_mask(e):
+            mask[e] = placed([P, C * 4], BF16, "mask%d" % e, at_mask[e])
+            nc.scalar.activation(mask[e][:], sign[e][:], ACT.Relu)
 
         def first_product(e):
             cols = slice(e * C, (e + 1) * C)
@@ -155,15 +176,15 @@ def tile_moe_adb_relu_kernel(
                 nc.tensor.matmul_mx(
                     out=sums[e][:],
                     lhsT=gw[s][:, cols].bitcast(FP8X4),
-                    lhsT_scale=gs[s][:, cols],
+                    lhsT_scale=gs[s][:, cols] if e < 4 else late[s][:, (e - 4) * C : (e - 3) * C],
                     rhs=wbw[e][:, s, :].bitcast(FP4X4),
-                    rhs_scale=wbs[e // 3][:, (e % 3) * PASSES + s, :],
+                    rhs_scale=wbs[e // 2][:, (e % 2) * PASSES + s, :],
                     start=(s == 0),
                     stop=(s == PASSES - 1),
                 )
 
         def apply_gate(e):
-            gated[e] = placed([P, H + 2 * C], BF16, "gated%d" % e, at_gated[e % 2])
+            gated[e] = placed([P, H], BF16, "gated%d" % e, at_gated[e])
             nc.scalar.activation(
                 gated[e][:, 0:H].rearrange("j (u p c) -> j u p c", u=2, c=2),
                 sums[e][:].rearrange("j (p u c) -> j u p c", u=2, c=2),
@@ -172,7 +193,7 @@ def tile_moe_adb_relu_kernel(
             )
 
         def turn(e):
-            turned[e] = bank_of(2, [P, 2, C]) if e == 0 else psum.tile([P, 2, C], F32, name="turned")
+            turned[e] = psum.tile([P, 2, C], F32, name="turned")
             for u in range(2):
                 nc.tensor.transpose(turned[e][:].rearrange("p u j -> p (u j)")[:, u : 2 * C : 2], gated[e][:].bitcast(F32)[:, u * P : (u + 1) * P], ident[:])
 
@@ -183,15 +204,12 @@ def tile_moe_adb_relu_kernel(
             )
 
         def quantize(e):
-            codes[e] = placed([P, C], U32, "codes%d" % e, at_gated[e % 2] + 2 * H)
-            if e == 0:
-                code_scales[e] = placed([P, C], U8, "code_scales0", at_mask[0])
-            else:
-                code_scales[e] = ring.tile([P, C], U8, name="code_scales", align_bytes=64)
+            codes[e] = ring.tile([P, C], U32, name="codes", align_bytes=64)
+            code_scales[e] = ring.tile([P, C], U8, name="code_scales", align_bytes=64)
             nc.vector.quantize_mx(out=codes[e][:].bitcast(FP8X4), scales=code_scales[e][:], in_=dh[e][:])
 
         def second_product(e):
-            dx_ps[e] = bank_of(e, [P, 2, C])
+            dx_ps[e] = bank_of(e + 1, [P, 2, C])
             for kt in range(2):
                 nc.tensor.matmul_mx(
                     out=dx_ps[e][:, kt, :],
@@ -203,12 +221,15 @@ def tile_moe_adb_relu_kernel(
                     stop=True,
                 )
 
-        def copy_dx(e):
-            dx[e] = placed([P, 2, C], F32, "dx%d" % e, at_gated[(e + 1) % 2])
-            nc.scalar.activation(dx[e][:], dx_ps[e][:], ACT.Copy)
+        def copy_dx(kt, e):
+            if kt == 1 and e + 2 < E:
+                dx[kt, e] = placed([P, C], F32, "dx1%d" % e, at_gated[e + 2])
+            else:
+                dx[kt, e] = held([P, C], F32, "dx%d%d" % (kt, e))
+            nc.scalar.activation(dx[kt, e][:], dx_ps[e][:, kt, :], ACT.Copy)
 
         def scatter(kt, e):
-            nc.vector.tensor_copy(win[kt][:].indirect(offsets[:, e * C // 16 : (e + 1) * C // 16]), dx[e][:, kt, :])
+            nc.vector.tensor_copy(win[kt][:].indirect(offsets[:, e * C // 16 : (e + 1) * C // 16]), dx[kt, e][:])
 
         def base(kt, h):
             bank = psum.tile([P, 512], F32, name="base%d%d" % (kt, h))
@@ -231,35 +252,40 @@ def tile_moe_adb_relu_kernel(
             nc.sync.dma_start(out[P * kt : P * (kt + 1), lo:hi], res[kt][:, lo:hi])
 
         for e in range(2):
+            make_sign(e)
             make_mask(e)
-        win.append(placed([P, T], F32, "win1", 12 * H))
-        clear(win[1])
-        load_scales(nc.gpsimd, wbs[1][:], wb_rows[:, :, 3 * PASSES :, :])
-        banks = {}
-        for e in range(2):
-            first_product(e)
-            apply_gate(e)
-            turn(e)
-        for e in range(E + 1):
-            if e < E:
-                apply_mask(e)
+        first_product(0)
+        apply_gate(0)
+        turn(0)
+        first_product(1)
+        for e in range(E):
+            apply_mask(e)
+            if e >= 2:
+                scatter(1, e - 2)
+            else:
+                gather_late(2 * e)
+            quantize(e)
             if e >= 1:
                 scatter(0, e - 1)
-            if e < E:
-                quantize(e)
-            if e >= 1:
-                scatter(1, e - 1)
-            if 1 <= e < E - 1:
+            else:
+                gather_late(1)
+            if e + 1 < E:
+                apply_gate(e + 1)
+                if e + 1 >= 2:
+                    make_mask(e + 1)
                 turn(e + 1)
-            if e < E:
-                second_product(e)
-                if e + 2 < E:
-                    first_product(e + 2)
-                copy_dx(e)
+            if e >= 1:
+                copy_dx(1, e - 1)
+            second_product(e)
             if e + 2 < E:
-                apply_gate(e + 2)
-                make_mask(e + 2)
-            if 2 <= e < E:
-                banks[divmod(e - 2, 2)] = base(*divmod(e - 2, 2))
+                make_sign(e + 2)
+            copy_dx(0, e)
+            if e + 2 < E:
+                first_product(e + 2)
+        copy_dx(1, E - 1)
+        scatter(1, E - 2)
+        scatter(0, E - 1)
+        scatter(1, E - 1)
+        banks = {(kt, h): base(kt, h) for kt in range(2) for h in range(2)}
         for kt, lo, hi in ((0, 0, 512), (0, 512, T), (1, 0, 512), (1, 512, 768), (1, 768, T)):
             finish(kt, lo, hi)

@@ -37,16 +37,18 @@ def tile_moe_adb_relu_kernel(
         def placed(shape, dtype, name, offset):
             return flow.tile(shape, dtype, name=name, align_bytes=64, offset=offset)
 
-        at_wb = [6 * H * e for e in range(E)]
-        at_gated = [6 * H * E + 2 * H * e for e in range(E)]
-        at_mask = [6 * H * E + 2 * H * E + 2 * H * e for e in range(2)] + at_wb[2:]
-        at_sign = [6 * H * E + 2 * H * (E + 2) + 2 * H * e for e in range(2)] + [at + 2 * H for at in at_wb[1:]]
+        row = 2 * H
+        at_wb = [PASSES * row * e for e in range(E)]
+        at_gated = [PASSES * row * E + row * e for e in range(E)]
+        at_free = PASSES * row * E + row * E
+        at_mask = [at_free] + at_wb[1:]
+        at_sign = [at_free + row, at_free + 2 * row] + [at + row for at in at_wb[1 : E - 1]]
 
         offsets = keep.tile([P, S // 16], U16, name="offsets")
         dyw = [held([P, T], I32, "dyw%d" % s) for s in range(PASSES)]
         dys = held([P, PASSES, T], U8, "dys")
         gw = [held([P, S], I32, "gw%d" % s) for s in range(PASSES)]
-        gs = [held([P, 4 * C], U8, "gs%d" % s) for s in range(PASSES)]
+        gs = [held([P, S], U8, "gs%d" % s) for s in range(PASSES)]
         wbs = [held([P, 2 * PASSES, H], U8, "wbs%d" % g) for g in range(3)]
         was = held([P, E, K], U8, "was")
         wts = held([P, PASSES, K], U8, "wts")
@@ -78,19 +80,20 @@ def tile_moe_adb_relu_kernel(
             nc.sync.dma_start(wbw[e][:].bitcast(I32), wbt_words[e].rearrange("s p b -> p s b").bitcast(I32))
 
         def load_wa(g):
-            waw[g] = held([P, 3, 2 * K], U8, "waw%d" % g)
-            rows = wat_words[3 * g : 3 * (g + 1)].rearrange("e s p b -> p (e s) b")
+            waw[g] = held([P, 2, 2 * K], U8, "waw%d" % g)
+            rows = wat_words[2 * g : 2 * (g + 1)].rearrange("e s p b -> p (e s) b")
             nc.sync.dma_start(waw[g][:].bitcast(I32), rows.bitcast(I32))
 
-        def load_a(g):
-            a_sb[g] = held([P, 4, 2 * C], F32, "a%d" % g)
-            nc.sync.dma_start(a_sb[g][:], a.rearrange("(p t) j -> p t j", t=4)[:, :, 2 * C * g : 2 * C * (g + 1)])
+        def load_a(first, last):
+            width = (last - first + 1) * C
+            saved = held([P, 4, width], F32, "a%d" % first)
+            nc.sync.dma_start(saved[:], a.rearrange("(p t) j -> p t j", t=4)[:, :, first * C : first * C + width])
+            for e in range(first, last + 1):
+                a_sb[e] = saved[:, :, (e - first) * C : (e - first + 1) * C]
 
         nc.sync.dma_start(offsets[:], offs)
         wb_rows = wbt_scales.rearrange("e s (q r) i -> r q (e s) i", r=4)
         for s in range(PASSES):
-            if s == PASSES - 1:
-                load_a(0)
             nc.sync.dma_start(dyw[s][:], dy_words[s].rearrange("p t d -> p (t d)").bitcast(I32))
         nc.sync.dma_start(gate_rows[0:E, :], gate.rearrange("p (e j) -> (p e) j", j=C)[0:E, :])
         load_scales(nc.sync, dys[:], dy_scales.rearrange("s (q r) t -> r q s t", r=4))
@@ -100,18 +103,21 @@ def tile_moe_adb_relu_kernel(
 
         load_wb_scales(0)
         load_wb(0)
+        load_a(0, 1)
         load_wb(1)
         load_wa(0)
         load_scales(nc.sync, was[:], wat_scales.rearrange("e s (q r) k -> r q (e s) k", r=4))
-        load_a(1)
+        load_a(2, 3)
         load_wb_scales(1)
         load_wb(2)
-        load_wb(3)
         load_wa(1)
-        load_a(2)
+        load_wb(3)
+        load_a(4, 4)
         load_wb_scales(2)
         load_wb(4)
         load_wb(5)
+        load_a(5, 5)
+        load_wa(2)
         load_scales(nc.gpsimd, wts[:], wt_scales.rearrange("s (q r) k -> r q s k", r=4), 4)
         wtw = held([P, PASSES, K], I32, "wtw")
         nc.sync.dma_start(wtw[:], wt_words.rearrange("s p k d -> p s (k d)").bitcast(I32))
@@ -127,33 +133,24 @@ def tile_moe_adb_relu_kernel(
         for kt in range(2):
             clear(win[kt])
 
-        def gather_words(s, lo, hi):
-            nc.vector.tensor_copy(
-                gw[s][:, lo:hi].bitcast(U32), dyw[s][:].bitcast(U32).indirect(offsets[:, lo // 16 : hi // 16])
-            )
+        def gather_words(s):
+            nc.vector.tensor_copy(gw[s][:].bitcast(U32), dyw[s][:].bitcast(U32).indirect(offsets[:]))
 
-        def gather_scales(dst, s, lo, hi):
-            nc.vector.tensor_copy(dst, dys[:, s, :].indirect(offsets[:, lo // 16 : hi // 16]))
+        def gather_scales(s, lo, hi):
+            nc.vector.tensor_copy(gs[s][:, lo:hi], dys[:, s, :].indirect(offsets[:, lo // 16 : hi // 16]))
 
-        late = {}
+        def bank_of(turn_no, shape):
+            return psum.tile(shape, F32, name="bank%d" % (turn_no % 3))
 
-        def gather_late(s):
-            at = (at_gated[0] + H, at_mask[0], at_gated[1] + H)[s]
-            late[s] = placed([P, 2 * C], U8, "late%d" % s, at)
-            gather_scales(late[s][:], s, 4 * C, S)
-
-        def bank_of(e, shape):
-            return psum.tile(shape, F32, name="bank%d" % (e % 3))
-
-        gate_ps = psum.tile([P, 2, C], F32, name="turned")
-        nc.tensor.transpose(gate_ps[:, 0, :], gate_rows[:, 0:C], ident[:])
-        nc.scalar.activation(gate_col[:], gate_ps[:, 0, 0:E], ACT.Copy)
+        gate_ps = psum.tile([P, C], F32, name="turned")
+        nc.tensor.transpose(gate_ps[:], gate_rows[:], ident[:])
+        nc.scalar.activation(gate_col[:], gate_ps[:, 0:E], ACT.Copy)
 
         for s in range(PASSES):
-            gather_words(s, 0, S)
-        for lo, hi in ((0, C), (C, 2 * C), (2 * C, 4 * C)):
+            gather_words(s)
+        for lo, hi in ((0, 2 * C), (2 * C, S)):
             for s in range(PASSES):
-                gather_scales(gs[s][:, lo:hi], s, lo, hi)
+                gather_scales(s, lo, hi)
 
         sign, mask, sums, gated, turned, dh, codes, code_scales, dx_ps, dx = {}, {}, {}, {}, {}, {}, {}, {}, {}, {}
 
@@ -161,7 +158,7 @@ def tile_moe_adb_relu_kernel(
             sign[e] = placed([P, C * 4], BF16, "sign%d" % e, at_sign[e])
             nc.scalar.activation(
                 sign[e][:].rearrange("p (c i t) -> p c t i", i=4, t=4),
-                a_sb[e // 2][:, :, (e % 2) * C : (e % 2 + 1) * C].rearrange("p t (c i) -> p c t i", i=4),
+                a_sb[e].rearrange("p t (c i) -> p c t i", i=4),
                 ACT.Sign,
             )
 
@@ -176,7 +173,7 @@ def tile_moe_adb_relu_kernel(
                 nc.tensor.matmul_mx(
                     out=sums[e][:],
                     lhsT=gw[s][:, cols].bitcast(FP8X4),
-                    lhsT_scale=gs[s][:, cols] if e < 4 else late[s][:, (e - 4) * C : (e - 3) * C],
+                    lhsT_scale=gs[s][:, cols],
                     rhs=wbw[e][:, s, :].bitcast(FP4X4),
                     rhs_scale=wbs[e // 2][:, (e % 2) * PASSES + s, :],
                     start=(s == 0),
@@ -186,22 +183,21 @@ def tile_moe_adb_relu_kernel(
         def apply_gate(e):
             gated[e] = placed([P, H], BF16, "gated%d" % e, at_gated[e])
             nc.scalar.activation(
-                gated[e][:, 0:H].rearrange("j (u p c) -> j u p c", u=2, c=2),
+                gated[e][:].rearrange("j (u p c) -> j u p c", u=2, c=2),
                 sums[e][:].rearrange("j (p u c) -> j u p c", u=2, c=2),
                 ACT.Copy,
                 scale=gate_col[:, e : e + 1],
             )
 
         def turn(e):
-            turned[e] = psum.tile([P, 2, C], F32, name="turned")
+            turned[e] = psum.tile([P, 2 * C], F32, name="turned")
+            words = gated[e][:].bitcast(F32)
             for u in range(2):
-                nc.tensor.transpose(turned[e][:].rearrange("p u j -> p (u j)")[:, u : 2 * C : 2], gated[e][:].bitcast(F32)[:, u * P : (u + 1) * P], ident[:])
+                nc.tensor.transpose(turned[e][:, u : 2 * C : 2], words[:, u * P : (u + 1) * P], ident[:])
 
         def apply_mask(e):
             dh[e] = ring.tile([P, C * 4], BF16, name="dh", align_bytes=64)
-            nc.vector.tensor_tensor(
-                dh[e][:], turned[e][:].rearrange("p u j -> p (u j)").bitcast(BF16), mask[e][:], ALU.mult
-            )
+            nc.vector.tensor_tensor(dh[e][:], turned[e][:].bitcast(BF16), mask[e][:], ALU.mult)
 
         def quantize(e):
             codes[e] = ring.tile([P, C], U32, name="codes", align_bytes=64)
@@ -213,7 +209,7 @@ def tile_moe_adb_relu_kernel(
             for kt in range(2):
                 nc.tensor.matmul_mx(
                     out=dx_ps[e][:, kt, :],
-                    lhsT=waw[e // 3][:, e % 3, 2 * P * kt : 2 * P * (kt + 1)].bitcast(FP4X4),
+                    lhsT=waw[e // 2][:, e % 2, 2 * P * kt : 2 * P * (kt + 1)].bitcast(FP4X4),
                     lhsT_scale=was[:, e, P * kt : P * (kt + 1)],
                     rhs=codes[e][:].bitcast(FP8X4),
                     rhs_scale=code_scales[e][:],
@@ -232,7 +228,7 @@ def tile_moe_adb_relu_kernel(
             nc.vector.tensor_copy(win[kt][:].indirect(offsets[:, e * C // 16 : (e + 1) * C // 16]), dx[kt, e][:])
 
         def base(kt, h):
-            bank = psum.tile([P, 512], F32, name="base%d%d" % (kt, h))
+            bank = psum.tile([P, 512], F32, name=(("turned", "bank2"), ("bank1", "bank0"))[kt][h])
             cols = slice(512 * h, 512 * (h + 1))
             for s in range(PASSES):
                 nc.tensor.matmul_mx(
@@ -251,9 +247,9 @@ def tile_moe_adb_relu_kernel(
             nc.vector.tensor_tensor(res[kt][:, lo:hi], win[kt][:, lo:hi], bank, ALU.add)
             nc.sync.dma_start(out[P * kt : P * (kt + 1), lo:hi], res[kt][:, lo:hi])
 
-        for e in range(2):
-            make_sign(e)
-            make_mask(e)
+        make_sign(0)
+        make_mask(0)
+        make_sign(1)
         first_product(0)
         apply_gate(0)
         turn(0)
@@ -262,17 +258,12 @@ def tile_moe_adb_relu_kernel(
             apply_mask(e)
             if e >= 2:
                 scatter(1, e - 2)
-            else:
-                gather_late(2 * e)
             quantize(e)
             if e >= 1:
                 scatter(0, e - 1)
-            else:
-                gather_late(1)
             if e + 1 < E:
                 apply_gate(e + 1)
-                if e + 1 >= 2:
-                    make_mask(e + 1)
+                make_mask(e + 1)
                 turn(e + 1)
             if e >= 1:
                 copy_dx(1, e - 1)

@@ -20,6 +20,8 @@ FP4X4 = mybir.dt.float4_e2m1fn_x4
 ACT = mybir.ActivationFunctionType
 ALU = mybir.AluOpType
 
+PAIR = 2 * C
+
 
 def tile_moe_adb_relu_kernel(
     tc, dy_words, dy_scales, wt_words, wt_scales, wbt_words, wbt_scales, wat_words, wat_scales, a, gate, offs, out
@@ -28,7 +30,6 @@ def tile_moe_adb_relu_kernel(
     with ExitStack() as ctx:
         keep = ctx.enter_context(tc.tile_pool(name="keep", bufs=1))
         flow = ctx.enter_context(tc.tile_pool(name="flow", bufs=1))
-        ring = ctx.enter_context(tc.tile_pool(name="ring", bufs=3))
         psum = ctx.enter_context(tc.psum_pool(name="psum", bufs=1))
 
         def held(shape, dtype, name):
@@ -38,34 +39,28 @@ def tile_moe_adb_relu_kernel(
             return flow.tile(shape, dtype, name=name, align_bytes=64, offset=offset)
 
         row = 2 * H
-        at_wb = [PASSES * row * e for e in range(E)]
-        at_gated = [PASSES * row * E + row * e for e in range(E)]
-        at_free = PASSES * row * E + row * E
-        at_mask = [at_free] + at_wb[1:]
-        at_sign = [at_free + row, at_free + 2 * row] + [at + row for at in at_wb[1 : E - 1]]
+        at_wb = [PASSES * row * e for e in range(E + 1)]
+        at_gated = [at_wb[E] + 2 * row * e for e in range(E)]
 
         offsets = keep.tile([P, S // 16], U16, name="offsets")
         dyw = [held([P, T], I32, "dyw%d" % s) for s in range(PASSES)]
         dys = held([P, PASSES, T], U8, "dys")
-        gw = [held([P, S], I32, "gw%d" % s) for s in range(PASSES)]
-        gs = [held([P, S], U8, "gs%d" % s) for s in range(PASSES)]
         wbs = [held([P, 2 * PASSES, H], U8, "wbs%d" % g) for g in range(3)]
         was = held([P, E, K], U8, "was")
         wts = held([P, PASSES, K], U8, "wts")
+        gate_rows = held([P, C], F32, "gate_rows")
         gate_col = held([P, E], F32, "gate_col")
+        zeros = held([P, P], F32, "zeros")
         ident = held([P, P], F32, "ident")
+        win = [held([P, T], F32, "win%d" % kt) for kt in range(2)]
         res = [held([P, T], F32, "res%d" % kt) for kt in range(2)]
 
-        def zero(planes):
-            nc.vector.memset(planes.rearrange("p a b -> p (a b)").bitcast(I32), 0)
+        def words_of(planes):
+            return planes[:].rearrange("p a b -> p (a b)").bitcast(I32)
 
-        for planes in (dys, wbs[0]):
-            zero(planes[:])
-        gate_rows = held([P, C], F32, "gate_rows")
         nc.vector.memset(gate_rows[:], 0.0)
-        zeros = held([P, P], F32, "zeros")
-        for planes in (wts, wbs[1], was, wbs[2]):
-            nc.gpsimd.memset(planes[:].rearrange("p a b -> p (a b)").bitcast(I32), 0)
+        for planes in (dys, wbs[0], was, wbs[1], wts, wbs[2]):
+            nc.vector.memset(words_of(planes), 0)
         nc.gpsimd.memset(zeros[:], 0.0)
         make_identity(nc, ident[:])
 
@@ -73,109 +68,108 @@ def tile_moe_adb_relu_kernel(
             for r in range(4):
                 queue.dma_start(planes[first + r : P : 32].bitcast(I32), rows[r].bitcast(I32))
 
-        wbw, waw, a_sb = {}, {}, {}
+        wbw, waw = {}, {}
 
         def load_wb(e):
             wbw[e] = placed([P, PASSES, 2 * H], U8, "wbw%d" % e, at_wb[e])
             nc.sync.dma_start(wbw[e][:].bitcast(I32), wbt_words[e].rearrange("s p b -> p s b").bitcast(I32))
 
-        def load_wa(g):
-            waw[g] = held([P, 2, 2 * K], U8, "waw%d" % g)
-            rows = wat_words[2 * g : 2 * (g + 1)].rearrange("e s p b -> p (e s) b")
-            nc.sync.dma_start(waw[g][:].bitcast(I32), rows.bitcast(I32))
-
-        def load_a(first, last):
-            width = (last - first + 1) * C
-            saved = held([P, 4, width], F32, "a%d" % first)
-            nc.sync.dma_start(saved[:], a.rearrange("(p t) j -> p t j", t=4)[:, :, first * C : first * C + width])
+        def load_wa(first, last):
+            words = held([P, last - first + 1, 2 * K], U8, "waw%d" % first)
+            rows = wat_words[first : last + 1].rearrange("e s p b -> p (e s) b")
+            nc.sync.dma_start(words[:].bitcast(I32), rows.bitcast(I32))
             for e in range(first, last + 1):
-                a_sb[e] = saved[:, :, (e - first) * C : (e - first + 1) * C]
+                waw[e] = words[:, e - first, :]
 
         nc.sync.dma_start(offsets[:], offs)
         wb_rows = wbt_scales.rearrange("e s (q r) i -> r q (e s) i", r=4)
+        saved, wtw = {}, {}
+
+        def load_a(first, last):
+            width = (last - first + 1) * C
+            saved[first] = held([P, 4, width], F32, "a%d" % first)
+            rows = a.rearrange("(p t) j -> p t j", t=4)[:, :, first * C : first * C + width]
+            nc.sync.dma_start(saved[first][:], rows)
+
+        def load_wt(kt):
+            wtw[kt] = held([P, PASSES, P], I32, "wtw%d" % kt)
+            rows = wt_words[:, :, kt * P : (kt + 1) * P, :].rearrange("s p k d -> p s (k d)")
+            nc.sync.dma_start(wtw[kt][:], rows.bitcast(I32))
+
         for s in range(PASSES):
             nc.sync.dma_start(dyw[s][:], dy_words[s].rearrange("p t d -> p (t d)").bitcast(I32))
-        nc.sync.dma_start(gate_rows[0:E, :], gate.rearrange("p (e j) -> (p e) j", j=C)[0:E, :])
         load_scales(nc.sync, dys[:], dy_scales.rearrange("s (q r) t -> r q s t", r=4))
-
-        def load_wb_scales(g):
-            load_scales(nc.sync, wbs[g][:], wb_rows[:, :, 2 * PASSES * g : 2 * PASSES * (g + 1), :])
-
-        load_wb_scales(0)
+        nc.sync.dma_start(gate_rows[0:E, :], gate.rearrange("p (e j) -> (p e) j", j=C)[0:E, :])
         load_wb(0)
-        load_a(0, 1)
+        load_scales(nc.sync, wbs[0][:], wb_rows[:, :, 0 : 2 * PASSES, :])
         load_wb(1)
-        load_wa(0)
+        load_a(0, 1)
         load_scales(nc.sync, was[:], wat_scales.rearrange("e s (q r) k -> r q (e s) k", r=4))
-        load_a(2, 3)
-        load_wb_scales(1)
         load_wb(2)
-        load_wa(1)
+        load_scales(nc.sync, wbs[1][:], wb_rows[:, :, 2 * PASSES : 4 * PASSES, :])
         load_wb(3)
-        load_a(4, 4)
-        load_wb_scales(2)
+        load_wa(0, 1)
+        load_a(2, 3)
+        load_scales(nc.sync, wts[:], wt_scales.rearrange("s (q r) k -> r q s k", r=4), 4)
+        load_wt(0)
         load_wb(4)
+        load_scales(nc.sync, wbs[2][:], wb_rows[:, :, 4 * PASSES :, :])
         load_wb(5)
-        load_a(5, 5)
-        load_wa(2)
-        load_scales(nc.gpsimd, wts[:], wt_scales.rearrange("s (q r) k -> r q s k", r=4), 4)
-        wtw = held([P, PASSES, K], I32, "wtw")
-        nc.sync.dma_start(wtw[:], wt_words.rearrange("s p k d -> p s (k d)").bitcast(I32))
+        load_wa(2, 3)
+        load_a(4, 5)
+        load_wa(4, 5)
+        load_wt(1)
 
-        def clear(window):
+        for kt in range(2):
             nc.scalar.activation(
-                window[:].rearrange("p (a b) -> p a b", b=P),
+                win[kt][:].rearrange("p (a b) -> p a b", b=P),
                 zeros[:].unsqueeze(1).to_broadcast([P, T // P, P]),
                 ACT.Copy,
             )
-
-        win = [held([P, T], F32, "win%d" % kt) for kt in range(2)]
-        for kt in range(2):
-            clear(win[kt])
-
-        def gather_words(s):
-            nc.vector.tensor_copy(gw[s][:].bitcast(U32), dyw[s][:].bitcast(U32).indirect(offsets[:]))
-
-        def gather_scales(s, lo, hi):
-            nc.vector.tensor_copy(gs[s][:, lo:hi], dys[:, s, :].indirect(offsets[:, lo // 16 : hi // 16]))
-
-        def bank_of(turn_no, shape):
-            return psum.tile(shape, F32, name="bank%d" % (turn_no % 3))
 
         gate_ps = psum.tile([P, C], F32, name="turned")
         nc.tensor.transpose(gate_ps[:], gate_rows[:], ident[:])
         nc.scalar.activation(gate_col[:], gate_ps[:, 0:E], ACT.Copy)
 
-        for s in range(PASSES):
-            gather_words(s)
-        for lo, hi in ((0, 2 * C), (2 * C, S)):
-            for s in range(PASSES):
-                gather_scales(s, lo, hi)
+        def tile_at(shape, dtype, name, at):
+            return held(shape, dtype, name) if at is None else placed(shape, dtype, name, at)
 
-        sign, mask, sums, gated, turned, dh, codes, code_scales, dx_ps, dx = {}, {}, {}, {}, {}, {}, {}, {}, {}, {}
+        gw, gs = {}, {}
 
-        def make_sign(e):
-            sign[e] = placed([P, C * 4], BF16, "sign%d" % e, at_sign[e])
-            nc.scalar.activation(
-                sign[e][:].rearrange("p (c i t) -> p c t i", i=4, t=4),
-                a_sb[e].rearrange("p t (c i) -> p c t i", i=4),
-                ACT.Sign,
+        def gather_words(s, lo, hi, at=None):
+            tile = tile_at([P, hi - lo], I32, "gw%d_%d" % (s, lo), at)
+            nc.vector.tensor_copy(tile[:].bitcast(U32), dyw[s][:].bitcast(U32).indirect(offsets[:, lo // 16 : hi // 16]))
+            for e in range(lo // C, hi // C):
+                gw[s, e] = tile[:, e * C - lo : (e + 1) * C - lo]
+
+        def gather_scales(s, lo, hi, at=None):
+            tile = tile_at([P, hi - lo], U8, "gs%d_%d" % (s, lo), at)
+            nc.vector.tensor_copy(tile[:], dys[:, s, :].indirect(offsets[:, lo // 16 : hi // 16]))
+            for e in range(lo // C, hi // C):
+                gs[s, e] = tile[:, e * C - lo : (e + 1) * C - lo]
+
+        mask, sums, gated, turned, dh, codes, code_scales = {}, {}, {}, {}, {}, {}, {}
+
+        def make_mask(first, count):
+            mask[first] = held([P, count * C * 4], BF16, "mask%d" % first)
+            nc.vector.tensor_single_scalar(
+                mask[first][:].rearrange("p (c i t) -> p c t i", i=4, t=4),
+                saved[first][:].rearrange("p t (c i) -> p c t i", i=4),
+                0.0,
+                ALU.is_gt,
             )
 
-        def make_mask(e):
-            mask[e] = placed([P, C * 4], BF16, "mask%d" % e, at_mask[e])
-            nc.scalar.activation(mask[e][:], sign[e][:], ACT.Relu)
-
         def first_product(e):
-            cols = slice(e * C, (e + 1) * C)
-            sums[e] = bank_of(e, [P, H])
+            sums[e] = psum.tile([P, H], F32, name="sums%d" % (e % 2))
+            planes = wbs[e // 2]
+            first = PASSES * (e % 2)
             for s in range(PASSES):
                 nc.tensor.matmul_mx(
                     out=sums[e][:],
-                    lhsT=gw[s][:, cols].bitcast(FP8X4),
-                    lhsT_scale=gs[s][:, cols],
+                    lhsT=gw[s, e].bitcast(FP8X4),
+                    lhsT_scale=gs[s, e],
                     rhs=wbw[e][:, s, :].bitcast(FP4X4),
-                    rhs_scale=wbs[e // 2][:, (e % 2) * PASSES + s, :],
+                    rhs_scale=planes[:, first + s, :],
                     start=(s == 0),
                     stop=(s == PASSES - 1),
                 )
@@ -189,51 +183,67 @@ def tile_moe_adb_relu_kernel(
                 scale=gate_col[:, e : e + 1],
             )
 
-        def turn(e):
-            turned[e] = psum.tile([P, 2 * C], F32, name="turned")
+        def turn(e, first, count, bank):
+            if e == first:
+                turned[first] = psum.tile([P, count, 2 * C], F32, name=bank)
             words = gated[e][:].bitcast(F32)
             for u in range(2):
-                nc.tensor.transpose(turned[e][:, u : 2 * C : 2], words[:, u * P : (u + 1) * P], ident[:])
+                nc.tensor.transpose(turned[first][:, e - first, u : 2 * C : 2], words[:, u * P : (u + 1) * P], ident[:])
 
-        def apply_mask(e):
-            dh[e] = ring.tile([P, C * 4], BF16, name="dh", align_bytes=64)
-            nc.vector.tensor_tensor(dh[e][:], turned[e][:].bitcast(BF16), mask[e][:], ALU.mult)
+        def apply_mask(first, count):
+            dh[first] = held([P, count * C * 4], BF16, "dh%d" % first)
+            lo = (first % 2) * C * 4
+            nc.vector.tensor_tensor(
+                dh[first][:],
+                turned[first][:].rearrange("p e w -> p (e w)").bitcast(BF16),
+                mask[first - first % 2][:, lo : lo + count * C * 4],
+                ALU.mult,
+            )
 
-        def quantize(e):
-            codes[e] = ring.tile([P, C], U32, name="codes", align_bytes=64)
-            code_scales[e] = ring.tile([P, C], U8, name="code_scales", align_bytes=64)
-            nc.vector.quantize_mx(out=codes[e][:].bitcast(FP8X4), scales=code_scales[e][:], in_=dh[e][:])
+        def quantize(first, count, at=None):
+            words = tile_at([P, count * C], U32, "codes%d" % first, at)
+            planes = held([P, count * C], U8, "code_scales%d" % first)
+            nc.vector.quantize_mx(out=words[:].bitcast(FP8X4), scales=planes[:], in_=dh[first][:])
+            for e in range(first, first + count):
+                codes[e] = words[:, (e - first) * C : (e - first + 1) * C]
+                code_scales[e] = planes[:, (e - first) * C : (e - first + 1) * C]
 
-        def second_product(e):
-            dx_ps[e] = bank_of(e + 1, [P, 2, C])
-            for kt in range(2):
+        def second_product(bank, parts):
+            sums_dx = psum.tile([P, 2, C], F32, name=bank)
+            for n, (kt, e) in enumerate(parts):
                 nc.tensor.matmul_mx(
-                    out=dx_ps[e][:, kt, :],
-                    lhsT=waw[e // 2][:, e % 2, 2 * P * kt : 2 * P * (kt + 1)].bitcast(FP4X4),
+                    out=sums_dx[:, n, :],
+                    lhsT=waw[e][:, 2 * P * kt : 2 * P * (kt + 1)].bitcast(FP4X4),
                     lhsT_scale=was[:, e, P * kt : P * (kt + 1)],
-                    rhs=codes[e][:].bitcast(FP8X4),
-                    rhs_scale=code_scales[e][:],
+                    rhs=codes[e].bitcast(FP8X4),
+                    rhs_scale=code_scales[e],
                     start=True,
                     stop=True,
                 )
+            return sums_dx
 
-        def copy_dx(kt, e):
-            if kt == 1 and e + 2 < E:
-                dx[kt, e] = placed([P, C], F32, "dx1%d" % e, at_gated[e + 2])
+        def copy_dx(bank, name, on_vector, at=None):
+            values = tile_at([P, 2, C], F32, name, at)
+            if on_vector:
+                nc.vector.tensor_copy(values[:], bank[:])
             else:
-                dx[kt, e] = held([P, C], F32, "dx%d%d" % (kt, e))
-            nc.scalar.activation(dx[kt, e][:], dx_ps[e][:, kt, :], ACT.Copy)
+                nc.scalar.activation(values[:], bank[:], ACT.Copy)
+            return values
 
-        def scatter(kt, e):
-            nc.vector.tensor_copy(win[kt][:].indirect(offsets[:, e * C // 16 : (e + 1) * C // 16]), dx[kt, e][:])
+        def scatter(kt, lo, hi, values, on_vector):
+            window = win[kt][:].indirect(offsets[:, lo // 16 : hi // 16])
+            if on_vector:
+                nc.vector.tensor_copy(window, values)
+            else:
+                nc.scalar.activation(window, values, ACT.Copy)
 
         def base(kt, h):
-            bank = psum.tile([P, 512], F32, name=(("turned", "bank2"), ("bank1", "bank0"))[kt][h])
+            bank = psum.tile([P, 512], F32, name=(("base0", "base1"), ("base2", "sums0"))[kt][h])
             cols = slice(512 * h, 512 * (h + 1))
             for s in range(PASSES):
                 nc.tensor.matmul_mx(
                     out=bank[:],
-                    lhsT=wtw[:, s, P * kt : P * (kt + 1)].bitcast(FP8X4),
+                    lhsT=wtw[kt][:, s, :].bitcast(FP8X4),
                     lhsT_scale=wts[4:P, s, P * kt : P * (kt + 1)],
                     rhs=dyw[s][:, cols].bitcast(FP8X4),
                     rhs_scale=dys[:, s, cols],
@@ -247,36 +257,65 @@ def tile_moe_adb_relu_kernel(
             nc.vector.tensor_tensor(res[kt][:, lo:hi], win[kt][:, lo:hi], bank, ALU.add)
             nc.sync.dma_start(out[P * kt : P * (kt + 1), lo:hi], res[kt][:, lo:hi])
 
-        make_sign(0)
-        make_mask(0)
-        make_sign(1)
-        first_product(0)
-        apply_gate(0)
-        turn(0)
-        first_product(1)
-        for e in range(E):
-            apply_mask(e)
-            if e >= 2:
-                scatter(1, e - 2)
-            quantize(e)
-            if e >= 1:
-                scatter(0, e - 1)
-            if e + 1 < E:
-                apply_gate(e + 1)
-                make_mask(e + 1)
-                turn(e + 1)
-            if e >= 1:
-                copy_dx(1, e - 1)
-            second_product(e)
-            if e + 2 < E:
-                make_sign(e + 2)
-            copy_dx(0, e)
-            if e + 2 < E:
-                first_product(e + 2)
-        copy_dx(1, E - 1)
-        scatter(1, E - 2)
-        scatter(0, E - 1)
-        scatter(1, E - 1)
+        def products(g):
+            first_product(2 * g)
+            first_product(2 * g + 1)
+
+        def front(first, count, bank="turned"):
+            for e in range(first, first + count):
+                apply_gate(e)
+                turn(e, first, count, bank)
+            if first % 2 == 0:
+                make_mask(first, 2)
+            apply_mask(first, count)
+
+        def pair_rows(first):
+            return [second_product("dx%d" % kt, [(kt, e) for e in (first, first + 1)]) for kt in range(2)]
+
+        def flat(values):
+            return values[:].rearrange("p e j -> p (e j)")
+
+        def both_rows(e):
+            return second_product("dx%d" % (e % 2), [(kt, e) for kt in range(2)])
+
+        for s in range(PASSES):
+            gather_words(s, 0, 2 * PAIR)
+        for lo in (0, PAIR):
+            for s in range(PASSES):
+                gather_scales(s, lo, lo + PAIR)
+        for s in range(2):
+            gather_scales(s, 2 * PAIR, S)
+        products(0)
+        front(0, 2)
+        gather_words(0, 2 * PAIR, S, at_gated[1] + row // 2)
+
+        products(1)
+        quantize(0, 2, at_wb[2])
+        banks_dx = pair_rows(0)
+        gather_words(1, 2 * PAIR, S, at_wb[2] + 2 * row)
+        gather_scales(2, 2 * PAIR, S, at_wb[2] + row + 2 * PAIR)
+        gather_words(2, 2 * PAIR, S, at_wb[3])
+        front(2, 2)
+        values = {kt: copy_dx(banks_dx[kt], "dx0_%d" % kt, False) for kt in (1, 0)}
+        scatter(1, 0, C, values[1][:, 0, :], False)
+        scatter(0, 0, PAIR, flat(values[0]), False)
+        scatter(1, C, PAIR, values[1][:, 1, :], True)
+
+        products(2)
+        quantize(2, 2, at_wb[4])
+        banks_dx = pair_rows(2)
+        front(4, 1)
+        front(5, 1, "sums1")
+        first_rows = copy_dx(banks_dx[0], "dx2_0", False)
+        second_rows = copy_dx(banks_dx[1], "dx2_1", False)
+        scatter(0, PAIR, 2 * PAIR, flat(first_rows), False)
+        scatter(1, PAIR, 2 * PAIR, flat(second_rows), False)
+        for e in (4, 5):
+            quantize(e, 1)
+        last = [copy_dx(both_rows(e), "dx%d" % e, True) for e in (4, 5)]
+        for kt in range(2):
+            for e in (4, 5):
+                scatter(kt, e * C, (e + 1) * C, last[e - 4][:, kt, :], kt == 0)
         banks = {(kt, h): base(kt, h) for kt in range(2) for h in range(2)}
         for kt, lo, hi in ((0, 0, 512), (0, 512, T), (1, 0, 512), (1, 512, 768), (1, 768, T)):
             finish(kt, lo, hi)

@@ -153,8 +153,8 @@ def tile_moe_adb_relu_kernel(
         def make_mask(first, count):
             mask[first] = held([P, count * C * 4], BF16, "mask%d" % first)
             nc.vector.tensor_single_scalar(
-                mask[first][:].rearrange("p (c i t) -> p c t i", i=4, t=4),
-                saved[first][:].rearrange("p t (c i) -> p c t i", i=4),
+                mask[first][:].rearrange("p (c i t) -> p c t i", i=2, t=4),
+                saved[first][:].rearrange("p t (c i) -> p c t i", i=2),
                 0.0,
                 ALU.is_gt,
             )

@@ -33,10 +33,10 @@ def tile_moe_adb_relu_kernel(
         psum = ctx.enter_context(tc.psum_pool(name="psum", bufs=1))
 
         def held(shape, dtype, name):
-            return keep.tile(shape, dtype, name=name, align_bytes=64)
+            return keep.tile(shape, dtype, name=name, align_bytes=256)
 
         def placed(shape, dtype, name, offset):
-            return flow.tile(shape, dtype, name=name, align_bytes=64, offset=offset)
+            return flow.tile(shape, dtype, name=name, align_bytes=256, offset=offset)
 
         row = 2 * H
         at_wb = [PASSES * row * e for e in range(E + 1)]

from contextlib import ExitStack

import concourse.mybir as mybir
from concourse.masks import make_identity

K, T, E, C, H, N = 256, 1024, 6, 128, 512, 1536
S = E * C
P = 128
PASSES = N // 512
FLOPS = 2 * N * K * T + 2 * N * H * S + 2 * H * K * S

F32 = mybir.dt.float32
BF16 = mybir.dt.bfloat16
I32 = mybir.dt.int32
U32 = mybir.dt.uint32
U16 = mybir.dt.uint16
U8 = mybir.dt.uint8
FP8X4 = mybir.dt.float8_e4m3fn_x4
FP4X4 = mybir.dt.float4_e2m1fn_x4
ACT = mybir.ActivationFunctionType
ALU = mybir.AluOpType

PAIR = 2 * C


def tile_moe_adb_relu_kernel(
    tc, dy_words, dy_scales, wt_words, wt_scales, wbt_words, wbt_scales, wat_words, wat_scales, a, gate, offs, out
):
    nc = tc.nc
    with ExitStack() as ctx:
        keep = ctx.enter_context(tc.tile_pool(name="keep", bufs=1))
        flow = ctx.enter_context(tc.tile_pool(name="flow", bufs=1))
        psum = ctx.enter_context(tc.psum_pool(name="psum", bufs=1))

        def held(shape, dtype, name):
            return keep.tile(shape, dtype, name=name, align_bytes=256)

        def placed(shape, dtype, name, offset):
            return flow.tile(shape, dtype, name=name, align_bytes=256, offset=offset)

        row = 2 * H
        at_wb = [PASSES * row * e for e in range(E + 1)]
        at_gated = [at_wb[E] + 2 * row * e for e in range(E)]

        offsets = keep.tile([P, S // 16], U16, name="offsets")
        dyw = [held([P, T], I32, "dyw%d" % s) for s in range(PASSES)]
        dys = held([P, PASSES, T], U8, "dys")
        wbs = [held([P, 2 * PASSES, H], U8, "wbs%d" % g) for g in range(3)]
        was = held([P, E, K], U8, "was")
        wts = held([P, PASSES, K], U8, "wts")
        gate_rows = held([P, C], F32, "gate_rows")
        gate_col = held([P, E], F32, "gate_col")
        zeros = held([P, P], F32, "zeros")
        ident = held([P, P], F32, "ident")
        win = [held([P, T], F32, "win%d" % kt) for kt in range(2)]
        res = [held([P, T], F32, "res%d" % kt) for kt in range(2)]

        def words_of(planes):
            return planes[:].rearrange("p a b -> p (a b)").bitcast(I32)

        nc.vector.memset(gate_rows[:], 0.0)
        for planes in (dys, wbs[0], was, wbs[1], wts, wbs[2]):
            nc.vector.memset(words_of(planes), 0)
        nc.gpsimd.memset(zeros[:], 0.0)
        make_identity(nc, ident[:])

        def load_scales(queue, planes, rows, first=0):
            for r in range(4):
                queue.dma_start(planes[first + r : P : 32].bitcast(I32), rows[r].bitcast(I32))

        wbw, waw = {}, {}

        def load_wb(e):
            wbw[e] = placed([P, PASSES, 2 * H], U8, "wbw%d" % e, at_wb[e])
            nc.sync.dma_start(wbw[e][:].bitcast(I32), wbt_words[e].rearrange("s p b -> p s b").bitcast(I32))

        def load_wa(first, last):
            words = held([P, last - first + 1, 2 * K], U8, "waw%d" % first)
            rows = wat_words[first : last + 1].rearrange("e s p b -> p (e s) b")
            nc.sync.dma_start(words[:].bitcast(I32), rows.bitcast(I32))
            for e in range(first, last + 1):
                waw[e] = words[:, e - first, :]

        nc.sync.dma_start(offsets[:], offs)
        wb_rows = wbt_scales.rearrange("e s (q r) i -> r q (e s) i", r=4)
        saved, wtw = {}, {}

        def load_a(first, last):
            width = (last - first + 1) * C
            saved[first] = held([P, 4, width], F32, "a%d" % first)
            rows = a.rearrange("(p t) j -> p t j", t=4)[:, :, first * C : first * C + width]
            nc.sync.dma_start(saved[first][:], rows)

        def load_wt(kt):
            wtw[kt] = held([P, PASSES, P], I32, "wtw%d" % kt)
            rows = wt_words[:, :, kt * P : (kt + 1) * P, :].rearrange("s p k d -> p s (k d)")
            nc.sync.dma_start(wtw[kt][:], rows.bitcast(I32))

        for s in range(PASSES):
            nc.sync.dma_start(dyw[s][:], dy_words[s].rearrange("p t d -> p (t d)").bitcast(I32))
        load_scales(nc.sync, dys[:], dy_scales.rearrange("s (q r) t -> r q s t", r=4))
        nc.sync.dma_start(gate_rows[0:E, :], gate.rearrange("p (e j) -> (p e) j", j=C)[0:E, :])
        load_wb(0)
        load_scales(nc.sync, wbs[0][:], wb_rows[:, :, 0 : 2 * PASSES, :])
        load_wb(1)
        load_a(0, 1)
        load_scales(nc.sync, was[:], wat_scales.rearrange("e s (q r) k -> r q (e s) k", r=4))
        load_wb(2)
        load_scales(nc.sync, wbs[1][:], wb_rows[:, :, 2 * PASSES : 4 * PASSES, :])
        load_wb(3)
        load_wa(0, 1)
        load_a(2, 3)
        load_scales(nc.sync, wts[:], wt_scales.rearrange("s (q r) k -> r q s k", r=4), 4)
        load_wt(0)
        load_wb(4)
        load_scales(nc.sync, wbs[2][:], wb_rows[:, :, 4 * PASSES :, :])
        load_wb(5)
        load_wa(2, 3)
        load_a(4, 5)
        load_wa(4, 5)
        load_wt(1)

        for kt in range(2):
            nc.scalar.activation(
                win[kt][:].rearrange("p (a b) -> p a b", b=P),
                zeros[:].unsqueeze(1).to_broadcast([P, T // P, P]),
                ACT.Copy,
            )

        gate_ps = psum.tile([P, C], F32, name="turned")
        nc.tensor.transpose(gate_ps[:], gate_rows[:], ident[:])
        nc.scalar.activation(gate_col[:], gate_ps[:, 0:E], ACT.Copy)

        def tile_at(shape, dtype, name, at):
            return held(shape, dtype, name) if at is None else placed(shape, dtype, name, at)

        gw, gs = {}, {}

        def gather_words(s, lo, hi, at=None):
            tile = tile_at([P, hi - lo], I32, "gw%d_%d" % (s, lo), at)
            nc.vector.tensor_copy(tile[:].bitcast(U32), dyw[s][:].bitcast(U32).indirect(offsets[:, lo // 16 : hi // 16]))
            for e in range(lo // C, hi // C):
                gw[s, e] = tile[:, e * C - lo : (e + 1) * C - lo]

        def gather_scales(s, lo, hi, at=None):
            tile = tile_at([P, hi - lo], U8, "gs%d_%d" % (s, lo), at)
            nc.vector.tensor_copy(tile[:], dys[:, s, :].indirect(offsets[:, lo // 16 : hi // 16]))
            for e in range(lo // C, hi // C):
                gs[s, e] = tile[:, e * C - lo : (e + 1) * C - lo]

        mask, sums, gated, turned, dh, codes, code_scales = {}, {}, {}, {}, {}, {}, {}

        def make_mask(first, count):
            mask[first] = held([P, count * C * 4], BF16, "mask%d" % first)
            nc.vector.tensor_single_scalar(
                mask[first][:].rearrange("p (c i t) -> p c t i", i=2, t=4),
                saved[first][:].rearrange("p t (c i) -> p c t i", i=2),
                0.0,
                ALU.is_gt,
            )

        def first_product(e):
            sums[e] = psum.tile([P, H], F32, name="sums%d" % (e % 2))
            planes = wbs[e // 2]
            first = PASSES * (e % 2)
            for s in range(PASSES):
                nc.tensor.matmul_mx(
                    out=sums[e][:],
                    lhsT=gw[s, e].bitcast(FP8X4),
                    lhsT_scale=gs[s, e],
                    rhs=wbw[e][:, s, :].bitcast(FP4X4),
                    rhs_scale=planes[:, first + s, :],
                    start=(s == 0),
                    stop=(s == PASSES - 1),
                )

        def apply_gate(e):
            gated[e] = placed([P, H], BF16, "gated%d" % e, at_gated[e])
            nc.scalar.activation(
                gated[e][:].rearrange("j (u p c) -> j u p c", u=2, c=2),
                sums[e][:].rearrange("j (p u c) -> j u p c", u=2, c=2),
                ACT.Copy,
                scale=gate_col[:, e : e + 1],
            )

        def turn(e, first, count, bank):
            if e == first:
                turned[first] = psum.tile([P, count, 2 * C], F32, name=bank)
            words = gated[e][:].bitcast(F32)
            for u in range(2):
                nc.tensor.transpose(turned[first][:, e - first, u : 2 * C : 2], words[:, u * P : (u + 1) * P], ident[:])

        def apply_mask(first, count):
            dh[first] = held([P, count * C * 4], BF16, "dh%d" % first)
            lo = (first % 2) * C * 4
            nc.vector.tensor_tensor(
                dh[first][:],
                turned[first][:].rearrange("p e w -> p (e w)").bitcast(BF16),
                mask[first - first % 2][:, lo : lo + count * C * 4],
                ALU.mult,
            )

        def quantize(first, count, at=None):
            words = tile_at([P, count * C], U32, "codes%d" % first, at)
            planes = held([P, count * C], U8, "code_scales%d" % first)
            nc.vector.quantize_mx(out=words[:].bitcast(FP8X4), scales=planes[:], in_=dh[first][:])
            for e in range(first, first + count):
                codes[e] = words[:, (e - first) * C : (e - first + 1) * C]
                code_scales[e] = planes[:, (e - first) * C : (e - first + 1) * C]

        def second_product(bank, parts):
            sums_dx = psum.tile([P, 2, C], F32, name=bank)
            for n, (kt, e) in enumerate(parts):
                nc.tensor.matmul_mx(
                    out=sums_dx[:, n, :],
                    lhsT=waw[e][:, 2 * P * kt : 2 * P * (kt + 1)].bitcast(FP4X4),
                    lhsT_scale=was[:, e, P * kt : P * (kt + 1)],
                    rhs=codes[e].bitcast(FP8X4),
                    rhs_scale=code_scales[e],
                    start=True,
                    stop=True,
                )
            return sums_dx

        def copy_dx(bank, name, on_vector, at=None):
            values = tile_at([P, 2, C], F32, name, at)
            if on_vector:
                nc.vector.tensor_copy(values[:], bank[:])
            else:
                nc.scalar.activation(values[:], bank[:], ACT.Copy)
            return values

        def scatter(kt, lo, hi, values, on_vector):
            window = win[kt][:].indirect(offsets[:, lo // 16 : hi // 16])
            if on_vector:
                nc.vector.tensor_copy(window, values)
            else:
                nc.scalar.activation(window, values, ACT.Copy)

        def base(kt, h):
            bank = psum.tile([P, 512], F32, name=(("base0", "base1"), ("base2", "sums0"))[kt][h])
            cols = slice(512 * h, 512 * (h + 1))
            for s in range(PASSES):
                nc.tensor.matmul_mx(
                    out=bank[:],
                    lhsT=wtw[kt][:, s, :].bitcast(FP8X4),
                    lhsT_scale=wts[4:P, s, P * kt : P * (kt + 1)],
                    rhs=dyw[s][:, cols].bitcast(FP8X4),
                    rhs_scale=dys[:, s, cols],
                    start=(s == 0),
                    stop=(s == PASSES - 1),
                )
            return bank

        def finish(kt, lo, hi):
            bank = banks[kt, lo // 512][:, lo % 512 : (hi - 1) % 512 + 1]
            nc.vector.tensor_tensor(res[kt][:, lo:hi], win[kt][:, lo:hi], bank, ALU.add)
            nc.sync.dma_start(out[P * kt : P * (kt + 1), lo:hi], res[kt][:, lo:hi])

        def products(g):
            first_product(2 * g)
            first_product(2 * g + 1)

        def front(first, count, bank="turned"):
            for e in range(first, first + count):
                apply_gate(e)
                turn(e, first, count, bank)
            if first % 2 == 0:
                make_mask(first, 2)
            apply_mask(first, count)

        def pair_rows(first):
            return [second_product("dx%d" % kt, [(kt, e) for e in (first, first + 1)]) for kt in range(2)]

        def flat(values):
            return values[:].rearrange("p e j -> p (e j)")

        def both_rows(e):
            return second_product("dx%d" % (e % 2), [(kt, e) for kt in range(2)])

        for s in range(PASSES):
            gather_words(s, 0, 2 * PAIR)
        for lo in (0, PAIR):
            for s in range(PASSES):
                gather_scales(s, lo, lo + PAIR)
        for s in range(2):
            gather_scales(s, 2 * PAIR, S)
        products(0)
        front(0, 2)
        gather_words(0, 2 * PAIR, S, at_gated[1] + row // 2)

        products(1)
        quantize(0, 2, at_wb[2])
        banks_dx = pair_rows(0)
        gather_words(1, 2 * PAIR, S, at_wb[2] + 2 * row)
        gather_scales(2, 2 * PAIR, S, at_wb[2] + row + 2 * PAIR)
        gather_words(2, 2 * PAIR, S, at_wb[3])
        front(2, 2)
        values = {kt: copy_dx(banks_dx[kt], "dx0_%d" % kt, False) for kt in (1, 0)}
        scatter(1, 0, C, values[1][:, 0, :], False)
        scatter(0, 0, PAIR, flat(values[0]), False)
        scatter(1, C, PAIR, values[1][:, 1, :], True)

        products(2)
        quantize(2, 2, at_wb[4])
        banks_dx = pair_rows(2)
        front(4, 1)
        front(5, 1, "sums1")
        first_rows = copy_dx(banks_dx[0], "dx2_0", False)
        second_rows = copy_dx(banks_dx[1], "dx2_1", False)
        scatter(0, PAIR, 2 * PAIR, flat(first_rows), False)
        scatter(1, PAIR, 2 * PAIR, flat(second_rows), False)
        for e in (4, 5):
            quantize(e, 1)
        last = [copy_dx(both_rows(e), "dx%d" % e, True) for e in (4, 5)]
        for kt in range(2):
            for e in (4, 5):
                scatter(kt, e * C, (e + 1) * C, last[e - 4][:, kt, :], kt == 0)
        banks = {(kt, h): base(kt, h) for kt in range(2) for h in range(2)}
        for kt, lo, hi in ((0, 0, 512), (0, 512, T), (1, 0, 512), (1, 512, 768), (1, 768, T)):
            finish(kt, lo, hi)
